import numpy as np, ml_dtypes
CORES = [5,29,101,125,133,157,229,253]
N = 8
import mx_ref
BF = ml_dtypes.bfloat16
def gentries(a):
    return np.ascontiguousarray(a.reshape(8, 16, -1).transpose(0, 2, 1)).reshape(8, -1)
def gtable(e):
    e = np.asarray(e); return np.ascontiguousarray(e.reshape(8, -1, 16).transpose(0, 2, 1)).reshape(128, -1).astype(np.int32)
def gcols(t, e):
    v = np.concatenate([t.reshape(8, 16, -1, 4), np.zeros((8, 16, 1, 4), BF)], axis=2)
    return np.ascontiguousarray(np.stack([v[g][:, e[g]] for g in range(8)])).reshape(128, -1)
def tile(rs):
    return np.stack(rs, axis=2).reshape(128, -1).astype(BF)
def pick(q, e):
    c = np.concatenate([q[0].reshape(128, -1, 4), np.zeros((128, 1, 4), np.uint8)], axis=1); s = np.concatenate([q[1], np.ones((16, 1), np.uint8)], axis=1)
    return (np.ascontiguousarray(c[:, e].reshape(128, -1)), np.ascontiguousarray(s[:, e]))
def join(*qs):
    return (np.concatenate([q[0] for q in qs], axis=1), np.concatenate([q[1] for q in qs], axis=1))
def put(q, e, v):
    c, s = q[0].reshape(128, -1, 4).copy(), q[1].copy(); c[:, e] = v[0].reshape(128, -1, 4); s[:, e] = v[1]
    return (c.reshape(128, -1), s)
def pk(c, s):
    return (np.ascontiguousarray(c), mx_ref.live(s))
def emit(q):
    return q[0], q[1]
def packed(v, rng):
    q = [mx_ref.quantize(np.ascontiguousarray(v[r])) for r in range(N)]
    return np.stack([a for a, b in q]), np.stack([mx_ref.plane(b, rng) for a, b in q])
def values_of_codes():
    e, c = np.zeros((128, 128, 4), np.float32), np.zeros((128, 2, 4), np.uint8)
    e[np.arange(128), np.arange(128), 0] = 1
    c[:127, :, 0] = np.arange(256).reshape(2, 128).T[:127]
    return mx_ref.matmul(mx_ref.quantize(e.reshape(128, 512).astype(BF)), (c.reshape(128, 8), np.full((16, 2), 127, np.uint8))).T.reshape(-1).astype(np.float64)
CODE_VALUE, SCALE_VALUE = values_of_codes(), 2.0 ** (np.arange(256) - 127.0)
def decode(q):
    return (CODE_VALUE[q[0]].reshape(16, 8, -1, 4) * SCALE_VALUE[q[1]][:, None, :, None] + 0.0).reshape(128, -1).astype(np.float32)
def f(rng, *shape):
    return mx_ref.flush((rng.standard_normal(shape, dtype=np.float32) * np.exp2(rng.integers(-2, 3, shape[:-1] + (1,)))).astype(BF))
def wide(rng, *shape, cols=0):
    v = rng.standard_normal(shape, dtype=np.float32) * np.exp2(rng.integers(-12, 13, shape)).astype(np.float32)
    if cols: v *= np.repeat(np.exp2(rng.integers(-cols, cols + 1, shape[:-2] + (1, shape[-1] // 4))) * (rng.random(shape[:-2] + (1, shape[-1] // 4)) > 0.0625), 4, axis=-1).astype(np.float32)
    return mx_ref.flush(v.astype(BF))
C, I = 320, 12
DIST = [1, 2, 4]
def big(v):
    v = v.astype(np.float32)
    v[np.abs(v) < np.float32(2.0 ** -16)] = 0
    return v.astype(BF)
def alike(t):
    return np.stack([t] * N)
def lists(t):
    return {"li": np.stack([gtable(t[0][r]) for r in range(N)]), "ri": np.stack([gtable(t[1][r]) for r in range(N)])}
def drawn(rng):
    return lists(rng.integers(0, I, (2, N, 8, C)))
def layers(rng):
    return big(f(rng, 128, 2048)).reshape(8, 16, 4, 8, 16, 4)
def weights(rng, w):
    c, s = packed(alike(np.ascontiguousarray(w).reshape(128, 2048)), rng)
    return {"wc": c, "ws": alike(s[0])}
def setup_inputs(rng):
    return {"x": big(f(rng, N, 128, 4 * C)), "u": alike(np.array(f(rng, 128, 512))), "mid": alike(big(f(rng, 128, 4 * I * I))), "v": np.array(f(rng, N, 128, 512)), **drawn(rng), **weights(rng, layers(rng))}
def scorer(rng):
    u = np.array(f(rng, 128, 512)).reshape(128, 128, 4)
    u[:, ::16] = 0
    return u
def setup_inputs_few(rng):
    d = setup_inputs(rng)
    x = d["x"].reshape(N, 8, 16, C, 4)
    e = rng.permutation(N)
    for r in range(N):
        k = rng.permutation(np.array([0, 1, 2, 3, C // 2 - 1, C // 2, C - 1, C]))
        if r == e[0]: k[:] = 0
        if r == e[1]: k[:] = C
        for g in range(8):
            c = (-rng.integers(0, 2, C)).astype(np.float32)
            c[rng.permutation(C)[:k[g]]] = 1
            x[r, g, 0, :, 0] = c.astype(BF)
    u = scorer(rng)
    for h in range(0, 128, 16): u[h, h, 0] = 1.0
    t = rng.integers(0, I, (2, N, 8, C))
    t[:, e[0]] = I - 1
    t[:, e[1]] = 0
    t[:, e[2]] = rng.integers(0, I, (2, 8, 1))
    w = layers(rng)
    w[:, :, :, :, 0] = 0
    return {"x": x.reshape(N, 128, 4 * C), "u": alike(u.reshape(128, 512)), "mid": d["mid"], "v": d["v"], **lists(t), **weights(rng, w)}
def setup_inputs_near(rng):
    d = setup_inputs(rng)
    x = d["x"].reshape(N, 8, 16, C, 4)
    x[:, :, :8] = 0
    o = rng.permutation(N) % 4
    for r in range(N):
        s = rng.integers(-1, 2, (8, C)).astype(np.float32)
        if o[r] % 2 == 1: s = s[:, np.arange(C) // 16]
        if o[r] < 2: s = s * np.float32(2.0 ** -30)
        for g in rng.permutation(8)[:4]: s[g, rng.integers(C)] = 2.0 ** 29 * rng.choice([-1.0, 1.0])
        x[r, :, 0, :, 0] = s.astype(BF)
    u = scorer(rng)
    small = rng.permutation(8)[:4]
    for g in range(8): u[16 * g, 16 * g, 0] = 2.0 ** -30 if g in small else 1.0
    m = np.array(d["mid"][0]).reshape(8, 16, I * I, 4)
    m[:, :8] = 0
    m[:, 0, :, 0] = 2.0 ** -28
    w = layers(rng)
    w[:, :8] = 0
    w[:, :, :, :, :8] = 0
    return {"x": x.reshape(N, 128, 4 * C), "u": alike(u.reshape(128, 512)), "mid": alike(m.reshape(128, 4 * I * I)), "v": d["v"], **drawn(rng), **weights(rng, w)}
def setup_inputs_fine(rng):
    d = setup_inputs(rng)
    x = d["x"].reshape(N, 8, 16, C, 4)
    x[:, :, :8] = 0
    n = rng.integers(1, 15, (N, 8, C))
    o = rng.permutation(N) % 3
    a = np.stack([n, n + rng.integers(-1, 2, (N, 8, C))], axis=-1) * np.exp2(o - 17.0)[:, None, None, None]
    x[:, :, 0, :, :2] = a.astype(np.float32).astype(BF)
    x[:, :, 1, :, 0] = 1.96875
    x[:, :, 8, :, 0] = 1.0
    u = scorer(rng)
    for h in range(0, 128, 16):
        u[h, h, 0] = 1.0
        u[h, h, 1] = -1.0
    m = np.array(d["mid"][0]).reshape(8, 16, I * I, 4)
    m[:, :8] = 0
    m[:, 8, :, 0] = 1.0
    w = layers(rng)
    w[:, :, :, :, :9] = 0
    w[np.arange(8), 8, 0, np.arange(8), 1, 0] = -1.0
    return {"x": x.reshape(N, 128, 4 * C), "u": alike(u.reshape(128, 512)), "mid": alike(m.reshape(128, 4 * I * I)), "v": d["v"], **drawn(rng), **weights(rng, w)}
def setup_inputs_huge(rng):
    d = setup_inputs(rng)
    h = rng.permutation(8)
    x = -0.98 - 0.02 * rng.random((N, 8, 16, C, 4))
    x[:, h[4:]] = (0.75 + 0.1 * rng.random((N, 4, 16, C, 4))) * rng.choice([-1.0, 1.0], (N, 4, 1, C, 1))
    m = (0.75 + 0.1 * rng.random((8, 16, I * I, 4))) * rng.choice([-1.0, 1.0], (8, 1, I * I, 1))
    u = scorer(rng)
    for g in range(8):
        a = 16 * int(rng.choice(h[4:]))
        u[a:a + 16, 16 * g] = (2.0 ** 30 * (1 - 0.1 * rng.random((16, 4))) * rng.choice([-1.0, 1.0])).astype(np.float32).astype(BF)
    w = np.zeros((128, 4, 128, 4), np.float32)
    i = np.arange(128)
    for b in range(4): w[i, b, i, b] = -1
    return {"x": (2.0 ** 30 * x).astype(np.float32).astype(BF).reshape(N, 128, 4 * C), "u": alike(u.reshape(128, 512)), "mid": alike((2.0 ** 30 * m).astype(np.float32).astype(BF).reshape(128, 4 * I * I)), "v": d["v"], **drawn(rng), **weights(rng, w.astype(BF))}
def setup_inputs_spread(rng):
    d = setup_inputs(rng)
    d["x"] = big(wide(rng, N, 128, 4 * C, cols=6))
    d["mid"] = alike(big(wide(rng, 128, 4 * I * I)))
    return d
def check_inputs(d):
    b = []
    for k in ("x", "u", "mid", "v"):
        a = np.abs(d[k].astype(np.float32))
        if not (np.isfinite(a).all() and ((a == 0) | (a >= 2.0 ** -30) & (a <= 2.0 ** 30)).all()): b.append("a value of " + k)
    for k in ("li", "ri"):
        if not ((d[k] >= 0) & (d[k] < I)).all(): b.append("an entry of " + k)
    for k in ("u", "mid", "wc", "ws"):
        if (d[k] != d[k][:1]).any(): b.append(k + " isn't the same on all ranks")
    if ((d["wc"] & 0x7F) == 0x7F).any(): b.append("a code of wc that is no number")
    none, least, most = [emit(mx_ref.quantize(np.full((128, 16), k, np.float32).astype(BF)))[1][0, 0] for k in (0.0, 2.0 ** -30, 2.0 ** 30)]
    for r in range(N):
        s = mx_ref.live(d["ws"][r])
        if ((s != none) & ((s < least) | (s > most))).any(): b.append("a scale of ws")
    return b
def reference(x, u, mid, v, li, ri, wc, ws):
    qu = [mx_ref.quantize(u[r]) for r in range(N)]
    lay = [pk(wc[r], ws[r]) for r in range(N)]
    third = [decode(mx_ref.quantize(mid[r])).astype(BF) for r in range(N)]
    state = [mx_ref.quantize(x[r]) for r in range(N)]
    left = [gentries(li[r]) for r in range(N)]
    right = [gentries(ri[r]) for r in range(N)]
    mix = np.arange(C).reshape(2, C // 2).T.reshape(-1)
    for d in DIST:
        made, outl, outr = [], [], []
        for r in range(N):
            s = mx_ref.matmul(qu[r], state[r])[::16]
            o = np.argsort(~(s > 0), axis=1, kind="stable")
            l, h = o[:, ::2], o[:, 1::2]
            full = decode(state[r]).astype(BF)
            most = np.maximum(gcols(full, l).astype(np.float32), gcols(full, h).astype(np.float32))
            n = I * np.take_along_axis(right[r], l, axis=1) + np.take_along_axis(left[r], h, axis=1)
            z = mx_ref.quantize(((most + gcols(third[r], n).astype(np.float32)) * np.float32(0.5)).astype(BF))
            made.append(mx_ref.quantize(tile([mx_ref.matmul(pick(lay[r], np.arange(128 * b, 128 * b + 128)), z) * np.float32(0.03125) + most[:, b::4] for b in range(4)])))
            outl.append(np.take_along_axis(left[r], l, axis=1))
            outr.append(np.take_along_axis(right[r], h, axis=1))
        for r in range(N):
            e = (r - d) % N
            state[r] = pick(join(made[e], made[r]), mix)
            left[r] = np.concatenate([outl[e], outl[r]], axis=1)[:, mix]
            right[r] = np.concatenate([outr[e], outr[r]], axis=1)[:, mix]
    y, lr = np.zeros((N, 128, C), np.float32), np.zeros((N, 8, 2 * C), np.float32)
    oc, osc = np.zeros((N, 128, 4 * C), np.uint8), np.zeros((N, 16, C), np.uint8)
    for r in range(N):
        y[r] = mx_ref.matmul(mx_ref.quantize(v[r]), state[r])
        lr[r] = np.concatenate([left[r], right[r]], axis=1)
        oc[r], osc[r] = emit(state[r])
    return {"y": y, "lr": lr, "oc": oc, "osc": osc}

@@ -1,0 +1,475 @@
+from concourse.bass import DstId, RemoteDMATransfer, IndirectOffsetOnAxis
+from concourse.mybir import dt, AluOpType, ActivationFunctionType
+
+C, H, NI = 320, 160, 12
+NM = NI * NI
+DIST = [1, 2, 4]
+BF, F32, I32, U16, U8, X4 = "bfloat16", "float32", "int32", "uint16", "uint8", "float8_e4m3fn_x4"
+
+
+def _sb(n, d):
+    return ("sbuf", [128, n], d)
+
+
+SCRATCH = {
+    "ps": ("psum", [128, 4096], F32),
+    "xt": _sb(4 * C, BF), "ut": _sb(512, BF), "mt": _sb(4 * NM, BF), "vt": _sb(512, BF),
+    "xc": _sb(C, X4), "xs": _sb(C, U8), "uc0": _sb(128, X4), "us0": _sb(128, U8), "uc1": _sb(128, X4), "us1": _sb(128, U8),
+    "mc": _sb(NM, X4), "ms": _sb(NM, U8), "vc": _sb(128, X4), "vs": _sb(128, U8), "wq": _sb(512, X4), "wp": _sb(512, U8),
+    "eye": _sb(520, BF), "ec": _sb(512, X4), "es": _sb(512, U8),
+    "pp": _sb(2, I32), "ci": _sb(8, I32), "cf": _sb(16, F32), "c16": _sb(20, F32),
+    "t16": _sb(336, BF), "t4": _sb(H, BF), "mk": _sb(336, BF), "kp": _sb(H, BF), "mk4": _sb(H, BF), "kp4": _sb(H, BF),
+    "val1": _sb(C, BF), "val2": _sb(C, BF), "j1": _sb(20, F32), "j2": _sb(20, F32),
+    "uo": _sb(8, U16), "ro": _sb(40, U16), "fo": _sb(20, U16),
+    "stage": ("dram", [8, 2 * C], I32), "lr0": _sb(2 * C, I32),
+    "ff": _sb(4 * C, BF), "mh": _sb(4 * NM, BF),
+    "fl": _sb(C, BF), "cs1": _sb(C + 2, BF), "cs2": _sb(H + 2, BF), "hd": _sb(2 * C, BF), "tc": _sb(2, F32),
+    "nf": _sb(20, F32), "nx": _sb(40, F32), "x0": _sb(20, F32), "x1": _sb(20, F32), "pf": _sb(20, F32), "ek": _sb(40, F32),
+    "pos": _sb(20, U16), "oo": _sb(C, BF), "e1": _sb(C, BF), "e2": _sb(C, BF), "off": _sb(20, U16),
+    "nb": _sb(H, BF), "nn": _sb(H, BF), "n1": _sb(H, BF), "n2": _sb(H, BF), "noff": _sb(40, U16),
+    "ll": _sb(4 * H, BF), "ph": _sb(4 * H, BF), "p32": _sb(4 * H, BF), "zt": _sb(4 * H, BF), "zc": _sb(H, X4), "zs": _sb(H, U8),
+    "v32": _sb(4 * H, BF), "vv": _sb(4 * H, BF),
+    "ab0": _sb(2 * C, BF), "ab1": _sb(2 * C, BF), "ab2": _sb(2 * C, BF), "ab3": _sb(C, BF),
+    "sc1": _sb(C, X4), "sc2": _sb(C, X4), "sc3": _sb(C, X4), "ss1": _sb(C, U8), "ss2": _sb(C, U8), "ss3": _sb(C, U8),
+    "ms1": _sb(50, BF), "ms2": _sb(50, BF), "ml1": _sb(66, BF), "ml2": _sb(66, BF),
+    "tbo": _sb(20, BF), "tbr": _sb(20, BF), "lro": _sb(40, F32),
+    "pkc": _sb(C, X4), "pks": _sb(C, U8), "yy": _sb(C, F32),
+    "hi": _sb(H, BF), "hs": _sb(H, U8), "hc": _sb(H, X4), "ht": _sb(50, BF),
+}
+NDMA = 20
+SEMAPHORES = (["pe", "ve", "ac", "gp", "sent", "h0", "h1", "h2"] + ["d%d" % k for k in range(NDMA)]
+              + [a + str(k) for a in ("ai", "as", "at", "aq") for k in (1, 2, 3)])
+
+
+def _bits(engines):
+    m = 0
+    for e in engines:
+        m |= 1 << e
+    return m
+
+
+def _helpers(T, topo, src, dst):
+    h = [c for c in topo.cores_of(src) if T.rank_of(c) is None and topo.may_write(c, dst)]
+    h.sort(key=lambda c: topo.die(c) != topo.die(src))
+    return h[:2]
+
+
+def _raw(T, name, lo, hi):
+    a = T[name][:, lo:hi]
+    return a.bitcast(dt.uint8) if SCRATCH[name][2] == X4 else a
+
+
+def helper_program(g, core, T, topo):
+    n = len(T.cores)
+    for r in range(n):
+        src, dst = T.cores[r], T.cores[(r + DIST[0]) % n]
+        if topo.may_write(src, dst) or core not in _helpers(T, topo, src, dst):
+            continue
+        first = _helpers(T, topo, src, dst).index(core) == 0
+        half = len(topo.engines(src, core)) // 2
+        rid, pid = topo.addr(dst, core)
+        if first:
+            jobs = [("h0", ("hi", 0, H), ("ab1", 2 * H, 3 * H), "ai1"), ("h1", ("hs", 0, H), ("ss1", H, C), "as1"),
+                    ("h2", ("ht", 0, 50), ("ml1", 16, 66), "at1")]
+        else:
+            jobs = [("h0", ("hi", 0, H), ("ab1", 3 * H, 4 * H), "ai1"), ("h1", ("hc", 0, H), ("sc1", H, C), "aq1")]
+        for sem, a, b, far in jobs:
+            g.wait_ge(T.sem[sem], half)
+            g.remote_dma(_raw(T, *b), _raw(T, *a), T.sem[far], T.sem.sent, pid, rid, topo.mask(core, dst))
+        g.wait_ge(T.sem.sent, len(jobs) * len(topo.engines(core, dst)))
+
+
+def rank_program(g, core, T, topo):
+    rank = T.rank_of(core)
+    if rank is None:
+        return helper_program(g, core, T, topo)
+    n = len(T.cores)
+    A, ACT = AluOpType, ActivationFunctionType
+    Q = {"pe": g.tensor, "ve": g.vector, "ac": g.scalar, "gp": g, "sy": g.sync}
+    known = {q: {} for q in Q}
+    count = {"pe": 0, "ve": 0, "ac": 0, "gp": 0, "dma": 0, "sent": 0}
+    hist, last, waited = {}, {}, {}
+
+    def V(name, lo=0, hi=None, step=1):
+        return (name, lo, SCRATCH[name][1][1] if hi is None else hi, step)
+
+    def ap(v):
+        return T[v[0]][:, v[1]:v[2]] if v[3] == 1 else T[v[0]][:, v[1]:v[2]:v[3]]
+
+    def cols(v):
+        if v[0] == "ps":
+            return {v[1] // 512}
+        return set(range(v[1], v[2], v[3]))
+
+    def wait(q, toks):
+        need = {}
+        for t in toks:
+            if known[q].get(t[0], 0) < t[1] and need.get(t[0], (0, 0))[1] < t[1]:
+                need[t[0]] = t
+        for t in need.values():
+            if known[q].get(t[0], 0) < t[1]:
+                Q[q].wait_ge(T.sem[t[0]], t[1])
+                waited[t[0]] = max(waited.get(t[0], 0), t[1])
+                known[q][t[0]] = t[1]
+                for s, val in t[2].items():
+                    known[q][s] = max(known[q].get(s, 0), val)
+
+    def note(v, kind, tok, q):
+        hist.setdefault(v[0], []).append((cols(v), kind, tok, q))
+
+    def op(q, fn, reads, writes, dma=False):
+        deps = []
+        for v, w in [(v, False) for v in reads] + [(v, True) for v in writes]:
+            c = cols(v)
+            for hc, kind, tok, hq in hist.get(v[0], []):
+                if (w or kind == "w" or (v[0] == "ps" and hq != q)) and not c.isdisjoint(hc):
+                    deps.append(tok)
+        wait(q, deps)
+        ins = fn()
+        if ins is None:
+            return None
+        if dma:
+            sem, val = "d%d" % count["dma"], 16
+            count["dma"] += 1
+            ins.then_inc(T.sem[sem], 16)
+        else:
+            count[q] += 1
+            sem, val = q, count[q]
+            ins.then_inc(T.sem[sem], 1)
+        tok = (sem, val, dict(known[q]))
+        last[sem] = val
+        for v in reads:
+            note(v, "r", tok, q)
+        for v in writes:
+            note(v, "w", tok, q)
+        return tok
+
+    def arrives(v, sem, val):
+        last[sem] = val
+        note(v, "w", (sem, val, {}), "far")
+
+    def is_view(s):
+        return isinstance(s, tuple)
+
+    def sc(s):
+        return ap(s) if is_view(s) else s
+
+    def gat(win, off):
+        return ap(win).indirect(ap(off))
+
+    def memset(o, c):
+        op("ve", lambda: g.vector.memset(ap(o), c), [], [o])
+
+    def copy(o, i):
+        op("ve", lambda: g.vector.tensor_copy(ap(o), ap(i)), [i], [o])
+
+    def ts(o, i, s1, o0, s2=None, o1=None, off=None):
+        r = [i] + [s for s in (s1, s2, off) if is_view(s)]
+        src = (lambda: ap(i)) if off is None else (lambda: gat(i, off))
+        if o1 is None:
+            op("ve", lambda: g.vector.tensor_scalar(ap(o), src(), sc(s1), None, o0), r, [o])
+        else:
+            op("ve", lambda: g.vector.tensor_scalar(ap(o), src(), sc(s1), sc(s2), o0, o1), r, [o])
+
+    def tt(o, a, b, alu, off=None):
+        if off is None:
+            op("ve", lambda: g.vector.tensor_tensor(ap(o), ap(a), ap(b), alu), [a, b], [o])
+        else:
+            op("ve", lambda: g.vector.tensor_tensor(ap(o), gat(a, off), ap(b), alu), [a, b, off], [o])
+
+    def scan(o, a, b, init, o0, o1):
+        op("ve", lambda: g.vector.tensor_tensor_scan(ap(o), ap(a), ap(b), init, o0, o1), [a, b], [o])
+
+    def act(o, i, scale=None, off=None, bias=None):
+        r = [i] + [s for s in (off, bias) if s is not None]
+        src = (lambda: ap(i)) if off is None else (lambda: gat(i, off))
+        if bias is not None:
+            op("ac", lambda: g.scalar.activation(ap(o), src(), ACT.Identity, bias=ap(bias), scale=scale), r, [o])
+        elif scale is None:
+            op("ac", lambda: g.scalar.activation(ap(o), src(), ACT.Copy), r, [o])
+        else:
+            op("ac", lambda: g.scalar.activation(ap(o), src(), ACT.Copy, scale=scale), r, [o])
+
+    def quant(c, s, i):
+        op("ve", lambda: g.vector.quantize_mx(ap(c), ap(s), ap(i)), [i], [c, s])
+
+    def bank(b, w):
+        return V("ps", 512 * b, 512 * b + w)
+
+    def mm(b, lc, ls, rc, rs):
+        o = bank(b, rc[2] - rc[1])
+        op("pe", lambda: g.tensor.matmul_mx(ap(o), ap(lc), ap(ls), ap(rc), ap(rs), True, True), [lc, ls, rc, rs], [o])
+
+    def pick_codes(o, win, off):
+        op("ve", lambda: g.vector.tensor_copy(ap(o).bitcast(dt.uint32), ap(win).bitcast(dt.uint32).indirect(ap(off))), [win, off], [o])
+
+    def iota(o, pattern, base, cm):
+        if SCRATCH[o[0]][2] == I32:
+            op("gp", lambda: g.iota(ap(o), pattern, base, cm), [], [o])
+        else:
+            op("gp", lambda: g.iota(ap(o), pattern, base, cm, allow_small_or_imprecise_dtypes=True), [], [o])
+
+    def dma(q, out, in_, reads, writes):
+        return op(q, lambda: Q[q].dma_start(out, in_), reads, writes, dma=True)
+
+    def send(src, dst, to, sem, engines):
+        rid, pid = topo.addr(to, core)
+
+        def fn():
+            g.remote_dma(_raw(T, *dst[:3]), _raw(T, *src[:3]), T.sem[sem], T.sem.sent, pid, rid, _bits(engines))
+        op("gp", fn, [src], [])
+        count["sent"] += len(engines)
+
+    def col(k):
+        return V("cf", k, k + 1)
+
+    def E(b):
+        return V("ec", 128 * b, 128 * b + 128), V("es", 128 * b, 128 * b + 128)
+
+    xin = dma("sy", T.xt[:], T.x[:], [], [V("xt")])
+    dma("ac", T.ut[:], T.u[:], [], [V("ut")])
+    dma("ac", T.stage[:, 0:C], T.li[:], [], [V("stage", 0, C)])
+    dma("ac", T.stage[:, C:2 * C], T.ri[:], [], [V("stage", C, 2 * C)])
+    wait("sy", [xin])
+    dma("sy", T.mt[:], T.mid[:], [], [V("mt")])
+    dma("sy", T.wq[:].bitcast(dt.uint8), T.wc[:], [], [V("wq")])
+    dma("sy", T.wp[:], T.ws[:], [], [V("wp")])
+    dma("sy", T.vt[:], T.v[:], [], [V("vt")])
+
+    memset(V("eye"), 0.0)
+    iota(V("pp"), [[0, 2]], 0, 1)
+    diag = V("eye", 3, 515, 4)
+    op("gp", lambda: g.affine_select(ap(diag), ap(diag), [[1, 128]], A.not_equal, 1.0, 0, -1), [diag], [diag])
+    iota(V("c16"), [[16, 20]], 0, 0)
+    iota(V("t16"), [[0, 21], [1, 16]], 0, 0)
+    iota(V("val1"), [[1, C]], -H, 0)
+    iota(V("t4"), [[0, H // 4], [1, 4]], 0, 0)
+    p = V("pp", 0, 1)
+    ts(V("ci", 0, 1), p, 15, A.bitwise_and)
+    ts(V("ci", 1, 2), p, 2, A.arith_shift_right, 3, A.bitwise_and)
+    ts(V("ci", 2, 3), p, 3, A.bitwise_and)
+    ts(V("ci", 3, 4), p, 4, A.arith_shift_right)
+    ts(V("ci", 4, 5), p, 1, A.arith_shift_right, 7, A.bitwise_and)
+    ts(V("ci", 5, 6), p, 1, A.bitwise_and)
+    memset(V("cs1", 0, 2), -H / 16)
+    memset(V("cs2", 0, 2), 0.0)
+    copy(V("cf", 0, 6), V("ci", 0, 6))
+    for b in range(4):
+        quant(*E(b), V("eye", 3 - b, 515 - b))
+    copy(V("uo"), V("c16", 0, 8))
+    ts(V("j1"), V("c16"), col(0), A.add)
+    ts(col(6), col(0), 0.0, A.is_equal)
+    ts(col(7), col(0), 0.0, A.is_equal, -H / 16, A.add)
+    ts(V("mk"), V("t16"), col(0), A.is_equal)
+    gi = V("ci", 3, 4)
+    op("gp", lambda: g.indirect_dma_start(T.lr0[:], None, T.stage[:], IndirectOffsetOnAxis(ap=ap(gi), axis=0), bounds_check=7),
+       [V("stage"), gi], [V("lr0")], dma=True)
+    iota(V("val2"), [[C, 2], [1, H]], -240, 0)
+
+    quant(V("uc0"), V("us0"), V("ut"))
+    pick_codes(V("uc1"), V("uc0"), V("uo"))
+    act(V("us1"), V("us0"), off=V("uo"))
+    quant(V("xc"), V("xs"), V("xt"))
+    mm(4, V("uc1"), V("us1"), V("xc"), V("xs"))
+    for b in range(4):
+        mm(b, *E(b), V("xc"), V("xs"))
+    for b in range(4):
+        act(V("ff", C * b, C * b + C), bank(b, C), 0.5)
+    ts(V("kp"), V("t16", 0, H), col(0), A.not_equal)
+    ts(col(8), col(0), 20.0, A.mult)
+    ts(col(9), col(0), 20.0, A.mult, float(C), A.add)
+    ts(col(12), col(0), 0.0, A.is_equal, 16.0, A.mult)
+
+    def counts(w, cs, init, total):
+        ts(V("fl", 0, w), bank(4, w), 0.0, A.is_gt, 1.0 / 32, A.mult)
+        scan(V(cs, 2, w + 2), V("fl", 0, w), V("fl", 0, w), init, A.add, A.add)
+        scan(V("hd", w, 2 * w), V(cs, 1, w + 1), V("mk", 1, w + 1), 100.0, A.min, A.add)
+        total(V(cs, w + 1, w + 2))
+        scan(V("hd", 0, w), V(cs, 2, w + 2), V("mk", 1, w + 1), 100.0, A.min, A.add)
+
+    counts(C, "cs1", -H / 16, lambda t: ts(V("tc", 0, 1), t, col(6), A.add))
+    he = V("hd", C + 15, 2 * C, 16)
+    ts(V("x0"), he, V("tc", 0, 1), A.subtract, -16.0, A.mult)
+    tt(V("nf"), V("hd", 15, C, 16), he, A.is_equal)
+    tt(V("nx", 20, 40), V("x0"), V("j1"), A.add)
+    ts(V("nx", 0, 20), he, col(7), A.subtract, 16.0, A.mult)
+
+    for k in range(1, len(DIST) + 1):
+        end = k == len(DIST)
+        to, frm = T.cores[(rank + DIST[k - 1]) % n], T.cores[(rank - DIST[k - 1]) % n]
+        hop = None if topo.may_write(core, to) else _helpers(T, topo, core, to)
+        via = None if topo.may_write(frm, core) else _helpers(T, topo, frm, core)
+        assert k == 1 or (hop is None and via is None)
+        ab, nab, qc, qs = "ab%d" % (k - 1), "ab%d" % k, "sc%d" % k, "ss%d" % k
+        if k == 1:
+            fwin = [V("ff", C * b, C * b + C) for b in range(4)]
+            awin, bwin, vals, back, nf = V(ab, 0, C), V(ab, C, 2 * C), V("val1"), float(H), V("nf")
+        else:
+            fwin = [V("ff", s, s + 3 * H) for s in (0, H, 4 * H, 5 * H)]
+            awin, bwin, vals, back, nf = V(ab, 0, 3 * H), V(ab, H, 4 * H), V("val2"), 240.0, V("ml%d" % (k - 1), 6, 26)
+            tt(V("nx"), V("ml%d" % (k - 1), 26, 66), V("ek"), A.add)
+        tt(V("x1"), V("nx", 20, 40), nf, A.mult)
+        if k == 1:
+            ts(V("ro", 0, 20), V("c16"), 1.0 / 16, A.mult, col(8), A.add)
+        tt(V("pf"), V("x1"), V("nx", 0, 20), A.max)
+        if k == 1:
+            ts(V("ro", 20, 40), V("c16"), 1.0 / 16, A.mult, col(9), A.add)
+        copy(V("pos"), V("pf"))
+        if k == 1:
+            quant(V("mc"), V("ms"), V("mt"))
+            for b in range(4):
+                mm((5, 6, 7, 4)[b], *E(b), V("mc"), V("ms"))
+            for b in range(4):
+                act(V("mh", b, 4 * NM, 4), bank((5, 6, 7, 4)[b], NM), 0.5)
+        op("ve", lambda: g.vector.tensor_copy(gat(V("oo"), V("pos")), ap(vals)), [vals, V("pos")], [V("oo")])
+        for s in range(2):
+            scan(V("e1", H * s, H * s + H), V("oo", s, C, 2), V("mk", 0, H), 0.0, A.add, A.mult)
+        for s in range(2):
+            scan(V("e2", H * s, H * s + H), V("kp"), V("e1", H * s, H * s + H), 0.0, A.mult, A.add)
+        lo, ho = V("off", 0, 10), V("off", 10, 20)
+        ts(lo, V("e2", 15, H, 16), back, A.add)
+        ts(ho, V("e2", H + 15, C, 16), back, A.add)
+
+        def left(b):
+            act(V("ll", H * b, H * b + H), fwin[b], off=lo)
+
+        def larger(b):
+            tt(V("ph", b, 4 * H, 4), fwin[b], V("ll", H * b, H * b + H), A.max, off=ho)
+
+        def middle(step):
+            if step == 0:
+                tt(V("nn"), awin, V("nb"), A.add, off=ho)
+            elif step == 1:
+                scan(V("n1"), V("nn"), V("mk4"), 0.0, A.add, A.mult)
+            elif step == 2:
+                scan(V("n2"), V("kp4"), V("n1"), 0.0, A.mult, A.add)
+            else:
+                ts(V("noff"), V("n2", 3, H, 4), 4.0, A.mult, col(2), A.add)
+
+        def indices():
+            act(V(nab, 0, H), awin, off=lo)
+            act(V(nab, H, C), bwin, off=ho)
+
+        if k == 1:
+            op("ve", lambda: g.vector.tensor_copy(ap(V(ab)), gat(V("lr0"), V("ro"))), [V("lr0"), V("ro")], [V(ab)])
+            ts(V("mk4"), V("t4"), col(1), A.is_equal)
+            ts(V("kp4"), V("t4"), col(1), A.not_equal)
+            for b in range(3):
+                left(b)
+            act(V("nb"), bwin, float(NI), off=lo)
+            indices()
+            left(3)
+            larger(0)
+            larger(1)
+            middle(0)
+            larger(2)
+            middle(1)
+            middle(2)
+            larger(3)
+            middle(3)
+        else:
+            ts(V("nb"), bwin, float(NI), A.mult, off=lo)
+            for b in range(4):
+                left(b)
+            for b in range(4):
+                middle(b)
+                larger(b)
+            indices()
+        act(V("p32"), V("ph"), 64.0)
+        far = len(topo.engines(via[0] if via else frm, core))
+        if end:
+            dma("sy", T.tbo[:], T[nab][0:128:16, 0:C], [V(nab)], [V("tbo")])
+            send(V("tbo"), V("tbr"), to, "ai%d" % k, topo.engines(core, to))
+            arrives(V("tbr"), "ai%d" % k, far)
+        elif hop:
+            eng = topo.engines(core, hop[0])
+            eng = [eng[len(eng) // 2:], eng[:len(eng) // 2]]
+
+            def both():
+                tr = []
+                for s in range(2):
+                    rid, pid = topo.addr(hop[s], core)
+                    tr.append(RemoteDMATransfer(dst_ids=[DstId(rid=rid, pnc=pid)], dma_engine_mask=_bits(eng[s]), remote_sem=T.sem.h0,
+                                                src=T[nab][:, H * s:H * s + H], dst=T.hi[:]))
+                g.remote_dma_fused(tr, local_sem=T.sem.sent)
+            op("gp", both, [V(nab, 0, C)], [])
+            count["sent"] += len(eng[0]) + len(eng[1])
+        else:
+            send(V(nab, 0, C), V(nab, C, 2 * C), to, "ai%d" % k, topo.engines(core, to))
+        if not end:
+            arrives(V(nab, C, 2 * C), "ai%d" % k, 2 * far if via else far)
+        tt(V("zt"), V("mh"), V("ph"), A.add, off=V("noff"))
+        quant(V("zc"), V("zs"), V("zt"))
+        for b in range(4):
+            mm(b, V("wq", 128 * b, 128 * b + 128), V("wp", 128 * b, 128 * b + 128), V("zc"), V("zs"))
+        if k == 1:
+            ts(V("j2", 0, 10), V("j1", 0, 10), 2.0, A.mult, 1.0, A.add)
+            ts(V("j2", 10, 20), V("j1", 0, 10), 2.0, A.mult)
+        for b in range(4):
+            tt(V("v32", H * b, H * b + H), bank(b, H), V("p32", b, 4 * H, 4), A.add)
+            if b < 3:
+                act(V("vv", b, 4 * H, 4), V("v32", H * b, H * b + H), 1.0 / 32)
+            else:
+                ts(V("vv", b, 4 * H, 4), V("v32", H * b, H * b + H), 1.0 / 32, A.mult)
+        oc, os_, rc, rs = V(qc, 0, H), V(qs, 0, H), V(qc, H, C), V(qs, H, C)
+        quant(oc, os_, V("vv"))
+        if hop:
+            send(oc, V("hc"), hop[1], "h1", eng[1])
+            send(os_, V("hs"), hop[0], "h1", eng[0])
+        else:
+            send(os_, rs, to, "as%d" % k, topo.engines(core, to))
+            if end:
+                send(oc, rc, to, "aq%d" % k, topo.engines(core, to))
+        arrives(rs, "as%d" % k, far)
+        arrives(rc, "aq%d" % k, far)
+        if end:
+            break
+        ms, ml = "ms%d" % k, "ml%d" % k
+        mm(4, V("uc1"), V("us1"), oc, os_)
+        for b in range(4):
+            mm(b, *E(b), oc, os_)
+        counts(H, "cs2", 0.0, lambda t: act(V("tc", 1, 2), t, 16.0, bias=col(12)))
+        hb = V("hd", 15, 2 * H, 16)
+        act(V(ms, 30, 50), hb, -16.0, bias=V("tc", 1, 2))
+        ts(V(ms, 10, 30), hb, col(6), A.subtract, 16.0, A.mult)
+        tt(V(ms, 0, 10), V("hd", 15, H, 16), V("hd", H + 15, 2 * H, 16), A.is_equal)
+        if hop:
+            send(V(ms), V("ht"), hop[0], "h2", eng[0])
+        else:
+            send(V(ms), V(ml, 16, 66), to, "at%d" % k, topo.engines(core, to))
+            send(oc, rc, to, "aq%d" % k, topo.engines(core, to))
+        arrives(V(ml, 16, 66), "at%d" % k, far)
+        at = (0, H, 4 * H, 5 * H)
+        for b in range(4):
+            act(V("ff", at[b], at[b] + H), bank(b, H), 0.5)
+        for s in range(2):
+            copy(V("ek", 10 * s, 10 * s + 10), V(ms, 20, 30))
+            tt(V("ek", 20 + 10 * s, 30 + 10 * s), V(ms, 40, 50), V("j2", 10 * s, 10 * s + 10), A.add)
+        copy(V(ml, 6, 16), V(ms, 0, 10))
+        if k == 1:
+            quant(V("vc"), V("vs"), V("vt"))
+            ts(col(10), col(5), -float(H), A.mult, float(H), A.add)
+            tt(col(11), col(10), col(4), A.add)
+            ts(V("fo"), V("c16"), 0.5, A.mult, col(11), A.add)
+        for b in range(4):
+            mm(4 + b, *E(b), rc, rs)
+        for b in range(4):
+            act(V("ff", at[b] + 2 * H, at[b] + 3 * H), bank(4 + b, H), 0.5)
+
+    mm(4, V("vc"), V("vs"), oc, os_)
+    act(V("yy", 1, C, 2), bank(4, H))
+    copy(V("lro", 1, 40, 2), V("tbo"))
+    copy(V("lro", 0, 40, 2), V("tbr"))
+    dma("sy", T.lr[:], T.lro[:], [V("lro")], [])
+    act(V("pks"), V(qs), off=V("fo"))
+    for a in range(4):
+        dma("sy", T.osc[4 * a:4 * a + 4, 0:C], T.pks[32 * a:32 * a + 4, 0:C], [V("pks")], [])
+    pick_codes(V("pkc"), V(qc), V("fo"))
+    mm(5, V("vc"), V("vs"), rc, rs)
+    act(V("yy", 0, C, 2), bank(5, H))
+    dma("sy", T.oc[:], T.pkc[:].bitcast(dt.uint8), [V("pkc")], [])
+    dma("ac", T.y[:], T.yy[:], [V("yy")], [])
+    last["sent"] = count["sent"]
+    for s, val in last.items():
+        if waited.get(s, 0) < val:
+            g.wait_ge(T.sem[s], val)

@@ -4,7 +4,13 @@ from concourse.mybir import dt, AluOpType, ActivationFunctionType
 C, H, NI = 320, 160, 12
 NM = NI * NI
 DIST = [1, 2, 4]
-BF, F32, I32, U16, U8, X4 = "bfloat16", "float32", "int32", "uint16", "uint8", "float8_e4m3fn_x4"
+BF, F16, F32, I32, U16, U8, X4 = "bfloat16", "float16", "float32", "int32", "uint16", "uint8", "float8_e4m3fn_x4"
+UNIT = 1024.0
+LOW = -65536.0
+KEEP = 512.0
+WHOLE = 130.0
+NH = 4
+PIECE = C // NH
 
 
 def _sb(n, d):
@@ -17,28 +23,31 @@ SCRATCH = {
     "xc": _sb(C, X4), "xs": _sb(C, U8), "uc0": _sb(128, X4), "us0": _sb(128, U8), "uc1": _sb(128, X4), "us1": _sb(128, U8),
     "mc": _sb(NM, X4), "ms": _sb(NM, U8), "vc": _sb(128, X4), "vs": _sb(128, U8), "wq": _sb(512, X4), "wp": _sb(512, U8),
     "eye": _sb(520, BF), "ec": _sb(512, X4), "es": _sb(512, U8),
-    "pp": _sb(2, I32), "ci": _sb(8, I32), "cf": _sb(16, F32), "c16": _sb(20, F32),
-    "t16": _sb(336, BF), "t4": _sb(H, BF), "mk": _sb(336, BF), "kp": _sb(H, BF), "mk4": _sb(H, BF), "kp4": _sb(H, BF),
-    "val1": _sb(C, BF), "val2": _sb(C, BF), "j1": _sb(20, F32), "j2": _sb(20, F32),
-    "uo": _sb(8, U16), "ro": _sb(40, U16), "fo": _sb(20, U16),
+    "pp": _sb(2, I32), "ci": _sb(8, I32), "cf": _sb(20, F32), "c16": _sb(20, F32),
+    "t16": _sb(336, BF), "t4": _sb(H, BF), "mk": _sb(336, BF), "h16": _sb(H, BF), "h4": _sb(H, BF), "ha": _sb(H, BF), "hb": _sb(H, BF),
+    "val1": _sb(C, BF), "val2": _sb(C, BF), "j2": _sb(20, F32),
+    "uo": _sb(8, U16), "fo": _sb(20, U16),
     "stage": ("dram", [8, 2 * C], I32), "lr0": _sb(2 * C, I32),
     "ff": _sb(4 * C, BF), "mh": _sb(4 * NM, BF),
     "fl": _sb(C, BF), "cs1": _sb(C + 2, BF), "cs2": _sb(H + 2, BF), "hd": _sb(2 * C, BF), "tc": _sb(2, F32),
-    "nf": _sb(20, F32), "nx": _sb(40, F32), "x0": _sb(20, F32), "x1": _sb(20, F32), "pf": _sb(20, F32), "ek": _sb(40, F32),
-    "pos": _sb(20, U16), "oo": _sb(C, BF), "e1": _sb(C, BF), "e2": _sb(C, BF), "off": _sb(20, U16),
-    "nb": _sb(H, BF), "nn": _sb(H, BF), "n1": _sb(H, BF), "n2": _sb(H, BF), "noff": _sb(40, U16),
+    "ml0": _sb(80, F32), "d1": _sb(80, F32), "pf": _sb(80, F32), "tq": _sb(20, F32),
+    "pos": _sb(20, U16), "oo": _sb(C, BF), "ee": _sb(C, F16), "off": _sb(20, U16),
+    "pa": _sb(40, BF), "pb": _sb(40, F32), "pc": _sb(40, F32), "poff": _sb(20, U16),
+    "nb": _sb(H, BF), "nn": _sb(H, BF), "n2": _sb(H, F16), "noff": _sb(40, U16),
     "ll": _sb(4 * H, BF), "ph": _sb(4 * H, BF), "p32": _sb(4 * H, BF), "zt": _sb(4 * H, BF), "zc": _sb(H, X4), "zs": _sb(H, U8),
     "v32": _sb(4 * H, BF), "vv": _sb(4 * H, BF),
-    "ab0": _sb(2 * C, BF), "ab1": _sb(2 * C, BF), "ab2": _sb(2 * C, BF), "ab3": _sb(C, BF),
+    "ab1": _sb(2 * C, BF), "ab2": _sb(2 * C, BF), "ab3": _sb(C, BF),
     "sc1": _sb(C, X4), "sc2": _sb(C, X4), "sc3": _sb(C, X4), "ss1": _sb(C, U8), "ss2": _sb(C, U8), "ss3": _sb(C, U8),
-    "ms1": _sb(50, BF), "ms2": _sb(50, BF), "ml1": _sb(66, BF), "ml2": _sb(66, BF),
-    "tbo": _sb(20, BF), "tbr": _sb(20, BF), "lro": _sb(40, F32),
+    "ms1": _sb(80, BF), "ms2": _sb(80, BF), "ml1": _sb(80, BF), "ml2": _sb(80, BF),
+    "pk": _sb(H, BF), "pr": _sb(H, BF), "pq": _sb(H, BF),
+    "fold": ("dram", [128, 20], BF), "land": ("dram", [128, 20], BF), "tb": _sb(2 * C, BF), "lro": _sb(2 * C, F32),
     "pkc": _sb(C, X4), "pks": _sb(C, U8), "yy": _sb(C, F32),
-    "hi": _sb(H, BF), "hs": _sb(H, U8), "hc": _sb(H, X4), "ht": _sb(50, BF),
+    "hi": _sb(PIECE, BF), "hs1": _sb(H, U8), "hs2": _sb(H, U8), "hc": _sb(H // 2, X4), "ht": _sb(80, BF),
 }
-NDMA = 20
+NDMA = 24
 SEMAPHORES = (["pe", "ve", "ac", "gp", "sent", "h0", "h1", "h2"] + ["d%d" % k for k in range(NDMA)]
               + [a + str(k) for a in ("ai", "as", "at", "aq") for k in (1, 2, 3)])
+LIST, CODES_A, CODES_B, SCALES = range(NH)
 
 
 def _bits(engines):
@@ -48,35 +57,48 @@ def _bits(engines):
     return m
 
 
-def _helpers(T, topo, src, dst):
+def _helpers(T, topo, src):
+    dst = T.cores[(T.rank_of(src) + DIST[0]) % len(T.cores)]
     h = [c for c in topo.cores_of(src) if T.rank_of(c) is None and topo.may_write(c, dst)]
     h.sort(key=lambda c: topo.die(c) != topo.die(src))
-    return h[:2]
+    return h[:NH]
+
+
+def _spare(topo, src, near, far):
+    return [e for e in topo.engines(src, near) if e not in topo.engines(src, far)]
 
 
 def _raw(T, name, lo, hi):
-    a = T[name][:, lo:hi]
+    a = T[name][:, lo:hi] if SCRATCH[name][0] == "sbuf" else T[name][:]
     return a.bitcast(dt.uint8) if SCRATCH[name][2] == X4 else a
 
 
 def helper_program(g, core, T, topo):
     n = len(T.cores)
     for r in range(n):
-        src, dst = T.cores[r], T.cores[(r + DIST[0]) % n]
-        if topo.may_write(src, dst) or core not in _helpers(T, topo, src, dst):
+        src = T.cores[r]
+        if core not in _helpers(T, topo, src):
             continue
-        first = _helpers(T, topo, src, dst).index(core) == 0
-        half = len(topo.engines(src, core)) // 2
-        rid, pid = topo.addr(dst, core)
-        if first:
-            jobs = [("h0", ("hi", 0, H), ("ab1", 2 * H, 3 * H), "ai1"), ("h1", ("hs", 0, H), ("ss1", H, C), "as1"),
-                    ("h2", ("ht", 0, 50), ("ml1", 16, 66), "at1")]
+        role = _helpers(T, topo, src).index(core)
+        one, two = T.cores[(r + DIST[0]) % n], T.cores[(r + DIST[1]) % n]
+        full = len(topo.engines(src, core))
+        jobs = [("h0", full // NH, ("hi", 0, PIECE), ("ab1", C + PIECE * role, C + PIECE * role + PIECE), "ai1", one)]
+        if role == LIST:
+            jobs.append(("h1", full, ("ht", 0, 80), ("ml1", 0, 80), "at1", one))
+        elif role == SCALES:
+            jobs.append(("h1", full, ("hs1", 0, H), ("ss1", H, C), "as1", one))
         else:
-            jobs = [("h0", ("hi", 0, H), ("ab1", 3 * H, 4 * H), "ai1"), ("h1", ("hc", 0, H), ("sc1", H, C), "aq1")]
-        for sem, a, b, far in jobs:
-            g.wait_ge(T.sem[sem], half)
+            lo = H + (H // 2) * (role - CODES_A)
+            jobs.append(("h1", full // 2, ("hc", 0, H // 2), ("sc1", lo, lo + H // 2), "aq1", one))
+        if role == CODES_A:
+            jobs.append(("h2", len(_spare(topo, src, core, two)), ("hs2", 0, H), ("ss2", H, C), "as2", two))
+        sent = 0
+        for sem, val, a, b, far, dst in jobs:
+            rid, pid = topo.addr(dst, core)
+            g.wait_ge(T.sem[sem], val)
             g.remote_dma(_raw(T, *b), _raw(T, *a), T.sem[far], T.sem.sent, pid, rid, topo.mask(core, dst))
-        g.wait_ge(T.sem.sent, len(jobs) * len(topo.engines(core, dst)))
+            sent += len(topo.engines(core, dst))
+        g.wait_ge(T.sem.sent, sent)
 
 
 def rank_program(g, core, T, topo):
@@ -180,11 +202,11 @@ def rank_program(g, core, T, topo):
     def scan(o, a, b, init, o0, o1):
         op("ve", lambda: g.vector.tensor_tensor_scan(ap(o), ap(a), ap(b), init, o0, o1), [a, b], [o])
 
-    def act(o, i, scale=None, off=None, bias=None):
-        r = [i] + [s for s in (off, bias) if s is not None]
+    def act(o, i, scale=None, off=None, bias=None, func=None):
+        r = [i] + [s for s in (off, bias) if is_view(s)]
         src = (lambda: ap(i)) if off is None else (lambda: gat(i, off))
         if bias is not None:
-            op("ac", lambda: g.scalar.activation(ap(o), src(), ACT.Identity, bias=ap(bias), scale=scale), r, [o])
+            op("ac", lambda: g.scalar.activation(ap(o), src(), func or ACT.Identity, bias=sc(bias), scale=scale), r, [o])
         elif scale is None:
             op("ac", lambda: g.scalar.activation(ap(o), src(), ACT.Copy), r, [o])
         else:
@@ -220,30 +242,51 @@ def rank_program(g, core, T, topo):
         op("gp", fn, [src], [])
         count["sent"] += len(engines)
 
+    def spread(srcs, dst, tos, sem):
+        eng = topo.engines(core, tos[0])
+        w = len(eng) // len(tos)
+
+        def fn():
+            tr = []
+            for s, to in enumerate(tos):
+                rid, pid = topo.addr(to, core)
+                tr.append(RemoteDMATransfer(dst_ids=[DstId(rid=rid, pnc=pid)], dma_engine_mask=_bits(eng[w * s:w * s + w]),
+                                            remote_sem=T.sem[sem], src=_raw(T, *srcs[s][:3]), dst=_raw(T, *dst[:3])))
+            g.remote_dma_fused(tr, local_sem=T.sem.sent)
+        op("gp", fn, srcs, [])
+        count["sent"] += len(eng)
+
     def col(k):
         return V("cf", k, k + 1)
 
     def E(b):
         return V("ec", 128 * b, 128 * b + 128), V("es", 128 * b, 128 * b + 128)
 
-    xin = dma("sy", T.xt[:], T.x[:], [], [V("xt")])
+    def hold_pattern(o, t, start):
+        act(V("ha"), t, -1.0, bias=start, func=ACT.Relu)
+        act(V("hb"), V("ha"), 1.0, bias=-0.75, func=ACT.Square)
+        act(o, V("hb"), -2 * KEEP, bias=2 * KEEP * 0.5625)
+
     dma("ac", T.ut[:], T.u[:], [], [V("ut")])
+    xin = dma("sy", T.xt[:], T.x[:], [], [V("xt")])
     dma("ac", T.stage[:, 0:C], T.li[:], [], [V("stage", 0, C)])
     dma("ac", T.stage[:, C:2 * C], T.ri[:], [], [V("stage", C, 2 * C)])
     wait("sy", [xin])
-    dma("sy", T.mt[:], T.mid[:], [], [V("mt")])
+    min_ = dma("sy", T.mt[:], T.mid[:], [], [V("mt")])
+    wait("sy", [min_])
     dma("sy", T.wq[:].bitcast(dt.uint8), T.wc[:], [], [V("wq")])
     dma("sy", T.wp[:], T.ws[:], [], [V("wp")])
     dma("sy", T.vt[:], T.v[:], [], [V("vt")])
 
+    I16, I4, T4, FIRST, LAST, J1, START16, START4, NOFF, P20, P16, J2, FO = 0, 1, 2, 6, 7, 8, 9, 10, 11, 12, 13, 14, 15
     memset(V("eye"), 0.0)
     iota(V("pp"), [[0, 2]], 0, 1)
     diag = V("eye", 3, 515, 4)
     op("gp", lambda: g.affine_select(ap(diag), ap(diag), [[1, 128]], A.not_equal, 1.0, 0, -1), [diag], [diag])
     iota(V("c16"), [[16, 20]], 0, 0)
     iota(V("t16"), [[0, 21], [1, 16]], 0, 0)
-    iota(V("val1"), [[1, C]], -H, 0)
     iota(V("t4"), [[0, H // 4], [1, 4]], 0, 0)
+    iota(V("val1"), [[1, C]], -H, 0)
     p = V("pp", 0, 1)
     ts(V("ci", 0, 1), p, 15, A.bitwise_and)
     ts(V("ci", 1, 2), p, 2, A.arith_shift_right, 3, A.bitwise_and)
@@ -251,16 +294,24 @@ def rank_program(g, core, T, topo):
     ts(V("ci", 3, 4), p, 4, A.arith_shift_right)
     ts(V("ci", 4, 5), p, 1, A.arith_shift_right, 7, A.bitwise_and)
     ts(V("ci", 5, 6), p, 1, A.bitwise_and)
-    memset(V("cs1", 0, 2), -H / 16)
+    memset(V("cs1", 0, 2), -H * UNIT)
     memset(V("cs2", 0, 2), 0.0)
     copy(V("cf", 0, 6), V("ci", 0, 6))
     for b in range(4):
         quant(*E(b), V("eye", 3 - b, 515 - b))
     copy(V("uo"), V("c16", 0, 8))
-    ts(V("j1"), V("c16"), col(0), A.add)
-    ts(col(6), col(0), 0.0, A.is_equal)
-    ts(col(7), col(0), 0.0, A.is_equal, -H / 16, A.add)
-    ts(V("mk"), V("t16"), col(0), A.is_equal)
+    ts(col(FIRST), col(I16), 0.0, A.is_equal, 16.0, A.mult)
+    ts(col(LAST), col(I16), 15.0, A.is_equal, KEEP, A.mult)
+    ts(col(16), col(I4), 3.0, A.not_equal, -4 * KEEP, A.mult)
+    memset(V("d1"), LOW)
+    memset(V("ml0"), LOW)
+    memset(V("ms1"), LOW)
+    act(V("cf", START16, START4 + 1), V("cf", I16, I4 + 1), 1.0, bias=2.0)
+    act(col(J1), col(FIRST), 2.0, bias=col(I16))
+    act(col(NOFF), col(16), 1.0, bias=col(T4))
+    act(col(P20), col(LAST), 20.0, bias=20 * (H - KEEP) + WHOLE * (C - 1))
+    act(col(P16), col(LAST), 1.0, bias=H - KEEP - 7.5 + 16 * WHOLE)
+    ts(V("mk"), V("t16"), col(I16), A.is_equal, 16 * UNIT, A.mult)
     gi = V("ci", 3, 4)
     op("gp", lambda: g.indirect_dma_start(T.lr0[:], None, T.stage[:], IndirectOffsetOnAxis(ap=ap(gi), axis=0), bounds_check=7),
        [V("stage"), gi], [V("lr0")], dma=True)
@@ -269,66 +320,61 @@ def rank_program(g, core, T, topo):
     quant(V("uc0"), V("us0"), V("ut"))
     pick_codes(V("uc1"), V("uc0"), V("uo"))
     act(V("us1"), V("us0"), off=V("uo"))
+    hold_pattern(V("h16"), V("t16", 0, H), col(START16))
+    hold_pattern(V("h4"), V("t4"), col(START4))
+    memset(V("d1", 2, 80, 4), 0.0)
+    memset(V("ms1", 2, 40, 4), 0.0)
+    ts(V("d1", 0, 80, 4), V("c16"), col(J1), A.add, -float(H), A.add)
     quant(V("xc"), V("xs"), V("xt"))
     mm(4, V("uc1"), V("us1"), V("xc"), V("xs"))
     for b in range(4):
         mm(b, *E(b), V("xc"), V("xs"))
     for b in range(4):
         act(V("ff", C * b, C * b + C), bank(b, C), 0.5)
-    ts(V("kp"), V("t16", 0, H), col(0), A.not_equal)
-    ts(col(8), col(0), 20.0, A.mult)
-    ts(col(9), col(0), 20.0, A.mult, float(C), A.add)
-    ts(col(12), col(0), 0.0, A.is_equal, 16.0, A.mult)
+    memset(V("pa"), 0.0)
+    memset(V("pb"), 1.0 - C)
 
     def counts(w, cs, init, total):
-        ts(V("fl", 0, w), bank(4, w), 0.0, A.is_gt, 1.0 / 32, A.mult)
+        ts(V("fl", 0, w), bank(4, w), 0.0, A.is_gt, UNIT / 2, A.mult)
         scan(V(cs, 2, w + 2), V("fl", 0, w), V("fl", 0, w), init, A.add, A.add)
-        scan(V("hd", w, 2 * w), V(cs, 1, w + 1), V("mk", 1, w + 1), 100.0, A.min, A.add)
+        scan(V("hd", w, 2 * w), V(cs, 1, w + 1), V("mk", 1, w + 1), 1e6, A.min, A.add)
         total(V(cs, w + 1, w + 2))
-        scan(V("hd", 0, w), V(cs, 2, w + 2), V("mk", 1, w + 1), 100.0, A.min, A.add)
+        scan(V("hd", 0, w), V(cs, 2, w + 2), V("mk", 1, w + 1), 1e6, A.min, A.add)
 
-    counts(C, "cs1", -H / 16, lambda t: ts(V("tc", 0, 1), t, col(6), A.add))
+    counts(C, "cs1", -H * UNIT, lambda t: ts(V("tc", 0, 1), t, 1 / UNIT, A.mult))
     he = V("hd", C + 15, 2 * C, 16)
-    ts(V("x0"), he, V("tc", 0, 1), A.subtract, -16.0, A.mult)
-    tt(V("nf"), V("hd", 15, C, 16), he, A.is_equal)
-    tt(V("nx", 20, 40), V("x0"), V("j1"), A.add)
-    ts(V("nx", 0, 20), he, col(7), A.subtract, 16.0, A.mult)
+    ts(V("ml0", 1, 80, 4), he, -2 / UNIT, A.mult, V("tc", 0, 1), A.add)
+    ts(V("ml0", 3, 80, 4), he, 1 / UNIT, A.mult)
+    tt(V("ml0", 2, 80, 4), he, V("hd", 15, C, 16), A.subtract)
 
+    hop = _helpers(T, topo, core)
     for k in range(1, len(DIST) + 1):
         end = k == len(DIST)
         to, frm = T.cores[(rank + DIST[k - 1]) % n], T.cores[(rank - DIST[k - 1]) % n]
-        hop = None if topo.may_write(core, to) else _helpers(T, topo, core, to)
-        via = None if topo.may_write(frm, core) else _helpers(T, topo, frm, core)
-        assert k == 1 or (hop is None and via is None)
+        assert topo.may_write(core, to) == (k > 1) and len(hop) == NH
         ab, nab, qc, qs = "ab%d" % (k - 1), "ab%d" % k, "sc%d" % k, "ss%d" % k
         if k == 1:
             fwin = [V("ff", C * b, C * b + C) for b in range(4)]
-            awin, bwin, vals, back, nf = V(ab, 0, C), V(ab, C, 2 * C), V("val1"), float(H), V("nf")
+            awin, bwin, vals, back = V("lr0", 0, C), V("lr0", C, 2 * C), V("val1"), float(H)
         else:
             fwin = [V("ff", s, s + 3 * H) for s in (0, H, 4 * H, 5 * H)]
-            awin, bwin, vals, back, nf = V(ab, 0, 3 * H), V(ab, H, 4 * H), V("val2"), 240.0, V("ml%d" % (k - 1), 6, 26)
-            tt(V("nx"), V("ml%d" % (k - 1), 26, 66), V("ek"), A.add)
-        tt(V("x1"), V("nx", 20, 40), nf, A.mult)
-        if k == 1:
-            ts(V("ro", 0, 20), V("c16"), 1.0 / 16, A.mult, col(8), A.add)
-        tt(V("pf"), V("x1"), V("nx", 0, 20), A.max)
-        if k == 1:
-            ts(V("ro", 20, 40), V("c16"), 1.0 / 16, A.mult, col(9), A.add)
-        copy(V("pos"), V("pf"))
+            awin, bwin, vals, back = V(ab, 0, 3 * H), V(ab, H, 4 * H), V("val2"), 240.0
+        scan(V("pf"), V("ml%d" % (k - 1)), V("d1"), 0.0, A.add, A.max)
         if k == 1:
             quant(V("mc"), V("ms"), V("mt"))
+        ts(V("pos"), V("pf", 3, 80, 4), col(FIRST), A.subtract, float(H) if k == 1 else 0.0, A.add)
+        if k == 1:
             for b in range(4):
                 mm((5, 6, 7, 4)[b], *E(b), V("mc"), V("ms"))
             for b in range(4):
                 act(V("mh", b, 4 * NM, 4), bank((5, 6, 7, 4)[b], NM), 0.5)
         op("ve", lambda: g.vector.tensor_copy(gat(V("oo"), V("pos")), ap(vals)), [vals, V("pos")], [V("oo")])
         for s in range(2):
-            scan(V("e1", H * s, H * s + H), V("oo", s, C, 2), V("mk", 0, H), 0.0, A.add, A.mult)
-        for s in range(2):
-            scan(V("e2", H * s, H * s + H), V("kp"), V("e1", H * s, H * s + H), 0.0, A.mult, A.add)
+            scan(V("ee", H * s, H * s + H), V("h16"), V("oo", s, C, 2), 0.0, A.add, A.max)
+        held = V("ee", 15, C, 16)
+        ts(V("off"), held, col(LAST), A.add, back - KEEP, A.add)
         lo, ho = V("off", 0, 10), V("off", 10, 20)
-        ts(lo, V("e2", 15, H, 16), back, A.add)
-        ts(ho, V("e2", H + 15, C, 16), back, A.add)
+        li, hi = (V("poff", 0, 10), V("poff", 10, 20)) if k == 1 else (lo, ho)
 
         def left(b):
             act(V("ll", H * b, H * b + H), fwin[b], off=lo)
@@ -338,73 +384,61 @@ def rank_program(g, core, T, topo):
 
         def middle(step):
             if step == 0:
-                tt(V("nn"), awin, V("nb"), A.add, off=ho)
+                tt(V("nn"), awin, V("nb"), A.add, off=hi)
             elif step == 1:
-                scan(V("n1"), V("nn"), V("mk4"), 0.0, A.add, A.mult)
-            elif step == 2:
-                scan(V("n2"), V("kp4"), V("n1"), 0.0, A.mult, A.add)
+                scan(V("n2"), V("h4"), V("nn"), 0.0, A.add, A.max)
             else:
-                ts(V("noff"), V("n2", 3, H, 4), 4.0, A.mult, col(2), A.add)
+                ts(V("noff"), V("n2", 3, H, 4), 4.0, A.mult, col(NOFF), A.add)
 
         def indices():
-            act(V(nab, 0, H), awin, off=lo)
-            act(V(nab, H, C), bwin, off=ho)
+            act(V(nab, 0, H), awin, off=li)
+            act(V(nab, H, C), bwin, 16.0 if k == 1 else None, off=hi)
 
         if k == 1:
-            op("ve", lambda: g.vector.tensor_copy(ap(V(ab)), gat(V("lr0"), V("ro"))), [V("lr0"), V("ro")], [V(ab)])
-            ts(V("mk4"), V("t4"), col(1), A.is_equal)
-            ts(V("kp4"), V("t4"), col(1), A.not_equal)
-            for b in range(3):
-                left(b)
-            act(V("nb"), bwin, float(NI), off=lo)
-            indices()
-            left(3)
+            ts(V("pa", 1, 40, 2), held, col(P16), A.add, 1.0 / 16, A.mult)
+            ts(V("pb", 1, 40, 2), held, 20.0, A.mult, col(P20), A.add)
+            left(0)
+            left(1)
+            scan(V("pc"), V("pa"), V("pb"), 0.0, A.mult, A.add)
+            copy(V("poff"), V("pc", 1, 40, 2))
             larger(0)
+            left(2)
+            act(V("nb"), bwin, float(NI), off=li)
+            left(3)
             larger(1)
-            middle(0)
             larger(2)
+            middle(0)
+            larger(3)
             middle(1)
             middle(2)
-            larger(3)
-            middle(3)
         else:
-            ts(V("nb"), bwin, float(NI), A.mult, off=lo)
+            ts(V("nb"), bwin, NI / 16, A.mult, off=li)
             for b in range(4):
                 left(b)
             for b in range(4):
-                middle(b)
+                if b < 3:
+                    middle(b)
                 larger(b)
-            indices()
+        indices()
         act(V("p32"), V("ph"), 64.0)
-        far = len(topo.engines(via[0] if via else frm, core))
-        if end:
-            dma("sy", T.tbo[:], T[nab][0:128:16, 0:C], [V(nab)], [V("tbo")])
-            send(V("tbo"), V("tbr"), to, "ai%d" % k, topo.engines(core, to))
-            arrives(V("tbr"), "ai%d" % k, far)
-        elif hop:
-            eng = topo.engines(core, hop[0])
-            eng = [eng[len(eng) // 2:], eng[:len(eng) // 2]]
-
-            def both():
-                tr = []
-                for s in range(2):
-                    rid, pid = topo.addr(hop[s], core)
-                    tr.append(RemoteDMATransfer(dst_ids=[DstId(rid=rid, pnc=pid)], dma_engine_mask=_bits(eng[s]), remote_sem=T.sem.h0,
-                                                src=T[nab][:, H * s:H * s + H], dst=T.hi[:]))
-                g.remote_dma_fused(tr, local_sem=T.sem.sent)
-            op("gp", both, [V(nab, 0, C)], [])
-            count["sent"] += len(eng[0]) + len(eng[1])
-        else:
-            send(V(nab, 0, C), V(nab, C, 2 * C), to, "ai%d" % k, topo.engines(core, to))
-        if not end:
-            arrives(V(nab, C, 2 * C), "ai%d" % k, 2 * far if via else far)
+        far = len(topo.engines(hop[0] if k == 1 else core, to))
+        if k == 1:
+            spread([V(nab, PIECE * s, PIECE * s + PIECE) for s in range(NH)], V("hi"), hop, "h0")
+            arrives(V(nab, C, 2 * C), "ai1", NH * far)
+        elif end:
+            dma("sy", T.fold[:], T[nab][0:128:16, :], [V(nab)], [V("fold")])
+            dma("sy", T.tb[0:8, 0:C], T[nab][0:128:16, :], [V(nab)], [V("tb", 0, C)])
+            send(V("fold"), V("land"), to, "ai%d" % k, topo.engines(core, to))
+            arrives(V("land"), "ai%d" % k, far)
+            dma("sy", T.tb[0:8, C:2 * C], T.land[:], [V("land")], [V("tb", C, 2 * C)])
         tt(V("zt"), V("mh"), V("ph"), A.add, off=V("noff"))
         quant(V("zc"), V("zs"), V("zt"))
+        if 1 < k < len(DIST):
+            tt(V("pk"), V(nab, 0, H), V(nab, H, C), A.add)
+            send(V("pk"), V("pr"), to, "ai%d" % k, topo.engines(core, to))
+            arrives(V("pr"), "ai%d" % k, far)
         for b in range(4):
             mm(b, V("wq", 128 * b, 128 * b + 128), V("wp", 128 * b, 128 * b + 128), V("zc"), V("zs"))
-        if k == 1:
-            ts(V("j2", 0, 10), V("j1", 0, 10), 2.0, A.mult, 1.0, A.add)
-            ts(V("j2", 10, 20), V("j1", 0, 10), 2.0, A.mult)
         for b in range(4):
             tt(V("v32", H * b, H * b + H), bank(b, H), V("p32", b, 4 * H, 4), A.add)
             if b < 3:
@@ -413,44 +447,57 @@ def rank_program(g, core, T, topo):
                 ts(V("vv", b, 4 * H, 4), V("v32", H * b, H * b + H), 1.0 / 32, A.mult)
         oc, os_, rc, rs = V(qc, 0, H), V(qs, 0, H), V(qc, H, C), V(qs, H, C)
         quant(oc, os_, V("vv"))
-        if hop:
-            send(oc, V("hc"), hop[1], "h1", eng[1])
-            send(os_, V("hs"), hop[0], "h1", eng[0])
+        if k == 1:
+            spread([V(qc, 0, H // 2), V(qc, H // 2, H)], V("hc"), [hop[CODES_A], hop[CODES_B]], "h1")
+            send(os_, V("hs1"), hop[SCALES], "h1", topo.engines(core, hop[SCALES]))
         else:
-            send(os_, rs, to, "as%d" % k, topo.engines(core, to))
+            send(oc, rc, to, "aq%d" % k, topo.engines(core, to))
             if end:
-                send(oc, rc, to, "aq%d" % k, topo.engines(core, to))
+                send(os_, rs, to, "as%d" % k, topo.engines(core, to))
+            else:
+                send(os_, V("hs2"), hop[CODES_A], "h2", _spare(topo, core, hop[CODES_A], to))
         arrives(rs, "as%d" % k, far)
-        arrives(rc, "aq%d" % k, far)
+        arrives(rc, "aq%d" % k, 2 * far if k == 1 else far)
         if end:
             break
         ms, ml = "ms%d" % k, "ml%d" % k
         mm(4, V("uc1"), V("us1"), oc, os_)
         for b in range(4):
             mm(b, *E(b), oc, os_)
-        counts(H, "cs2", 0.0, lambda t: act(V("tc", 1, 2), t, 16.0, bias=col(12)))
+        counts(H, "cs2", 0.0, lambda t: act(V("tc", 1, 2), t, 1 / UNIT))
         hb = V("hd", 15, 2 * H, 16)
-        act(V(ms, 30, 50), hb, -16.0, bias=V("tc", 1, 2))
-        ts(V(ms, 10, 30), hb, col(6), A.subtract, 16.0, A.mult)
-        tt(V(ms, 0, 10), V("hd", 15, H, 16), V("hd", H + 15, 2 * H, 16), A.is_equal)
-        if hop:
-            send(V(ms), V("ht"), hop[0], "h2", eng[0])
+        act(V(ms, 1, 80, 4), hb, -2 / UNIT, bias=V("tc", 1, 2))
+        ts(V(ms, 3, 80, 4), hb, 1 / UNIT, A.mult)
+        tt(V(ms, 42, 80, 4), V("hd", H + 15, 2 * H, 16), V("hd", 15, H, 16), A.subtract)
+        if k == 1:
+            send(V(ms), V("ht"), hop[LIST], "h1", topo.engines(core, hop[LIST]))
         else:
-            send(V(ms), V(ml, 16, 66), to, "at%d" % k, topo.engines(core, to))
-            send(oc, rc, to, "aq%d" % k, topo.engines(core, to))
-        arrives(V(ml, 16, 66), "at%d" % k, far)
+            send(V(ms), V(ml), to, "at%d" % k, topo.engines(core, to))
+        arrives(V(ml), "at%d" % k, far)
         at = (0, H, 4 * H, 5 * H)
         for b in range(4):
             act(V("ff", at[b], at[b] + H), bank(b, H), 0.5)
-        for s in range(2):
-            copy(V("ek", 10 * s, 10 * s + 10), V(ms, 20, 30))
-            tt(V("ek", 20 + 10 * s, 30 + 10 * s), V(ms, 40, 50), V("j2", 10 * s, 10 * s + 10), A.add)
-        copy(V(ml, 6, 16), V(ms, 0, 10))
         if k == 1:
+            ts(col(17), col(FIRST), 1.5, A.mult, col(I16), A.add)
+            memset(V("ms2"), LOW)
+            ts(V("j2", 10, 20), V("c16", 0, 10), col(17), A.add, 2.0, A.mult)
+            memset(V("ms2", 2, 40, 4), 0.0)
+            ts(V("j2", 0, 10), V("j2", 10, 20), 1.0, A.add)
+        tt(V("tq", 0, 10), V(ms, 41, 80, 4), V(ms, 43, 80, 4), A.add)
+        for s in range(2):
+            ts(V("d1", 40 * s + 2, 40 * s + 40, 4), V(ms, 43, 80, 4), col(FIRST), A.subtract)
+        tt(V("d1", 40, 80, 4), V("tq", 0, 10), V("j2", 10, 20), A.add)
+        tt(V("tq", 10, 20), V("tq", 0, 10), V("j2", 0, 10), A.add)
+        tt(V("d1", 0, 40, 4), V("tq", 10, 20), V(ms, 42, 80, 4), A.add)
+        if k > 1:
+            ts(V("pq"), V("pr"), 2304.0 - NI / 2, A.add)
+            ts(V(nab, 3 * H, 4 * H), V("pq"), -2304.0, A.add)
+            tt(V(nab, 2 * H, 3 * H), V("pr"), V(nab, 3 * H, 4 * H), A.subtract)
+        if k == 1:
+            ts(col(18), col(5), -float(H), A.mult, float(H), A.add)
             quant(V("vc"), V("vs"), V("vt"))
-            ts(col(10), col(5), -float(H), A.mult, float(H), A.add)
-            tt(col(11), col(10), col(4), A.add)
-            ts(V("fo"), V("c16"), 0.5, A.mult, col(11), A.add)
+            tt(col(FO), col(18), col(4), A.add)
+            ts(V("fo"), V("c16"), 0.5, A.mult, col(FO), A.add)
         for b in range(4):
             mm(4 + b, *E(b), rc, rs)
         for b in range(4):
@@ -458,17 +505,19 @@ def rank_program(g, core, T, topo):
 
     mm(4, V("vc"), V("vs"), oc, os_)
     act(V("yy", 1, C, 2), bank(4, H))
-    copy(V("lro", 1, 40, 2), V("tbo"))
-    copy(V("lro", 0, 40, 2), V("tbr"))
-    dma("sy", T.lr[:], T.lro[:], [V("lro")], [])
-    act(V("pks"), V(qs), off=V("fo"))
-    for a in range(4):
-        dma("sy", T.osc[4 * a:4 * a + 4, 0:C], T.pks[32 * a:32 * a + 4, 0:C], [V("pks")], [])
+    for s in range(2):
+        for lo, at in ((H * s, C * s + 1), (C + H * s, C * s)):
+            op("ve", lambda: g.vector.tensor_scalar(T.lro[0:8, at:C * s + C:2], T.tb[0:8, lo:lo + H], (1.0, 1.0 / 16)[s], None, A.mult),
+               [V("tb", lo, lo + H)], [V("lro", at, C * s + C, 2)])
+    dma("sy", T.lr[:], T.lro[0:8, :], [V("lro")], [])
     pick_codes(V("pkc"), V(qc), V("fo"))
+    dma("sy", T.oc[:], T.pkc[:].bitcast(dt.uint8), [V("pkc")], [])
     mm(5, V("vc"), V("vs"), rc, rs)
     act(V("yy", 0, C, 2), bank(5, H))
-    dma("sy", T.oc[:], T.pkc[:].bitcast(dt.uint8), [V("pkc")], [])
     dma("ac", T.y[:], T.yy[:], [V("yy")], [])
+    op("ve", lambda: g.vector.tensor_copy(ap(V("pks")), gat(V(qs), V("fo"))), [V(qs), V("fo")], [V("pks")])
+    for a in range(4):
+        dma("sy", T.osc[4 * a:4 * a + 4, 0:C], T.pks[32 * a:32 * a + 4, 0:C], [V("pks")], [])
     last["sent"] = count["sent"]
     for s, val in last.items():
         if waited.get(s, 0) < val:

@@ -10,7 +10,7 @@ LOW = -65536.0
 KEEP = 512.0
 WHOLE = 130.0
 NH = 4
-PIECE = C // NH
+PLANES = (0, 2, 1, 3)
 
 
 def _sb(n, d):
@@ -24,7 +24,7 @@ SCRATCH = {
     "mc": _sb(NM, X4), "ms": _sb(NM, U8), "vc": _sb(128, X4), "vs": _sb(128, U8), "wq": _sb(512, X4), "wp": _sb(512, U8),
     "eye": _sb(520, BF), "ec": _sb(512, X4), "es": _sb(512, U8),
     "pp": _sb(2, I32), "ci": _sb(8, I32), "cf": _sb(20, F32), "c16": _sb(20, F32),
-    "t16": _sb(336, BF), "t4": _sb(H, BF), "mk": _sb(336, BF), "h16": _sb(H, BF), "h4": _sb(H, BF), "ha": _sb(H, BF), "hb": _sb(H, BF),
+    "t16": _sb(336, BF), "t8": _sb(H, BF), "mk": _sb(336, BF), "h16": _sb(H, BF), "h8": _sb(H, BF), "ha": _sb(H, BF), "hb": _sb(H, BF),
     "val1": _sb(C, BF), "val2": _sb(C, BF), "j2": _sb(20, F32),
     "uo": _sb(8, U16), "fo": _sb(20, U16),
     "stage": ("dram", [8, 2 * C], I32), "lr0": _sb(2 * C, I32),
@@ -33,19 +33,20 @@ SCRATCH = {
     "ml0": _sb(80, F32), "d1": _sb(80, F32), "pf": _sb(80, F32), "tq": _sb(20, F32),
     "pos": _sb(20, U16), "oo": _sb(C, BF), "ee": _sb(C, F16), "off": _sb(20, U16),
     "pa": _sb(40, BF), "pb": _sb(40, F32), "pc": _sb(40, F32), "poff": _sb(20, U16),
-    "nb": _sb(H, BF), "nn": _sb(H, BF), "n2": _sb(H, F16), "noff": _sb(40, U16),
+    "nb": _sb(H, BF), "nn": _sb(H, BF), "n2": _sb(H, F16), "noff": _sb(20, U16), "ro": _sb(20, U16), "ab0": _sb(2 * C, BF),
     "ll": _sb(4 * H, BF), "ph": _sb(4 * H, BF), "p32": _sb(4 * H, BF), "zt": _sb(4 * H, BF), "zc": _sb(H, X4), "zs": _sb(H, U8),
     "v32": _sb(4 * H, BF), "vv": _sb(4 * H, BF),
     "ab1": _sb(2 * C, BF), "ab2": _sb(2 * C, BF), "ab3": _sb(C, BF),
     "sc1": _sb(C, X4), "sc2": _sb(C, X4), "sc3": _sb(C, X4), "ss1": _sb(C, U8), "ss2": _sb(C, U8), "ss3": _sb(C, U8),
     "ms1": _sb(80, BF), "ms2": _sb(80, BF), "ml1": _sb(80, BF), "ml2": _sb(80, BF),
-    "pk": _sb(H, BF), "pr": _sb(H, BF), "pq": _sb(H, BF),
+    "out4": ("dram", [NH, 128, 10], I32), "hi": ("dram", [128, 10], I32), "in4": ("dram", [NH, 128, 10], I32),
+    "stage1": ("dram", [8, 2 * C], I32), "lr1": _sb(2 * C, I32), "ho": _sb(20, U16), "poff1": _sb(20, U16),
     "fold": ("dram", [128, 20], BF), "land": ("dram", [128, 20], BF), "tb": _sb(2 * C, BF), "lro": _sb(2 * C, F32),
     "pkc": _sb(C, X4), "pks": _sb(C, U8), "yy": _sb(C, F32),
-    "hi": _sb(PIECE, BF), "hs1": _sb(H, U8), "hs2": _sb(H, U8), "hc": _sb(H // 2, X4), "ht": _sb(80, BF),
+    "hs1": _sb(H, U8), "hs2": _sb(H, U8), "hc": _sb(H // 2, X4), "ht": _sb(80, BF),
 }
-NDMA = 24
-SEMAPHORES = (["pe", "ve", "ac", "gp", "sent", "h0", "h1", "h2"] + ["d%d" % k for k in range(NDMA)]
+NDMA = 28
+SEMAPHORES = (["pe", "ve", "ac", "gp", "sent", "h0", "h1", "h2", "h3", "ao"] + ["d%d" % k for k in range(NDMA)]
               + [a + str(k) for a in ("ai", "as", "at", "aq") for k in (1, 2, 3)])
 LIST, CODES_A, CODES_B, SCALES = range(NH)
 
@@ -69,7 +70,8 @@ def _spare(topo, src, near, far):
 
 
 def _raw(T, name, lo, hi):
-    a = T[name][:, lo:hi] if SCRATCH[name][0] == "sbuf" else T[name][:]
+    where, shape, _ = SCRATCH[name]
+    a = T[name][:, lo:hi] if where == "sbuf" else T[name][:] if len(shape) == 2 else T[name][lo]
     return a.bitcast(dt.uint8) if SCRATCH[name][2] == X4 else a
 
 
@@ -82,10 +84,11 @@ def helper_program(g, core, T, topo):
         role = _helpers(T, topo, src).index(core)
         one, two = T.cores[(r + DIST[0]) % n], T.cores[(r + DIST[1]) % n]
         full = len(topo.engines(src, core))
-        jobs = [("h0", full // NH, ("hi", 0, PIECE), ("ab1", C + PIECE * role, C + PIECE * role + PIECE), "ai1", one)]
+        jobs = [("h0", full // NH, ("hi", 0, 10), ("in4", role, role + 1), "ai1", one)]
         if role == LIST:
             jobs.append(("h1", full, ("ht", 0, 80), ("ml1", 0, 80), "at1", one))
         elif role == SCALES:
+            jobs.append(("h3", full, ("ho", 0, 20), ("poff1", 0, 20), "ao", one))
             jobs.append(("h1", full, ("hs1", 0, H), ("ss1", H, C), "as1", one))
         else:
             lo = H + (H // 2) * (role - CODES_A)
@@ -267,10 +270,12 @@ def rank_program(g, core, T, topo):
         act(V("hb"), V("ha"), 1.0, bias=-0.75, func=ACT.Square)
         act(o, V("hb"), -2 * KEEP, bias=2 * KEEP * 0.5625)
 
+    dma("ac", T.stage[:, 0:C], T.li[:], [], [V("stage", 0, C)])
+    dma("sy", T.stage[:, C:2 * C], T.ri[:], [], [V("stage", C, 2 * C)])
     dma("ac", T.ut[:], T.u[:], [], [V("ut")])
     xin = dma("sy", T.xt[:], T.x[:], [], [V("xt")])
-    dma("ac", T.stage[:, 0:C], T.li[:], [], [V("stage", 0, C)])
-    dma("ac", T.stage[:, C:2 * C], T.ri[:], [], [V("stage", C, 2 * C)])
+    dma("ac", T.out4[0:2], T.li[:], [], [V("out4", 0, 2)])
+    dma("ac", T.out4[2:4], T.ri[:], [], [V("out4", 2, 4)])
     wait("sy", [xin])
     min_ = dma("sy", T.mt[:], T.mid[:], [], [V("mt")])
     wait("sy", [min_])
@@ -278,76 +283,93 @@ def rank_program(g, core, T, topo):
     dma("sy", T.wp[:], T.ws[:], [], [V("wp")])
     dma("sy", T.vt[:], T.v[:], [], [V("vt")])
 
-    I16, I4, T4, FIRST, LAST, J1, START16, START4, NOFF, P20, P16, J2, FO = 0, 1, 2, 6, 7, 8, 9, 10, 11, 12, 13, 14, 15
+    I16, I8, T2, I20, FIRST, LAST, J1, START16, START8, NOFF, P20, P16, FO = 0, 1, 2, 5, 6, 7, 8, 9, 10, 11, 12, 13, 15
     memset(V("eye"), 0.0)
     iota(V("pp"), [[0, 2]], 0, 1)
+    iota(V("c16"), [[16, 20]], 0, 0)
     diag = V("eye", 3, 515, 4)
     op("gp", lambda: g.affine_select(ap(diag), ap(diag), [[1, 128]], A.not_equal, 1.0, 0, -1), [diag], [diag])
-    iota(V("c16"), [[16, 20]], 0, 0)
     iota(V("t16"), [[0, 21], [1, 16]], 0, 0)
-    iota(V("t4"), [[0, H // 4], [1, 4]], 0, 0)
-    iota(V("val1"), [[1, C]], -H, 0)
     p = V("pp", 0, 1)
-    ts(V("ci", 0, 1), p, 15, A.bitwise_and)
-    ts(V("ci", 1, 2), p, 2, A.arith_shift_right, 3, A.bitwise_and)
-    ts(V("ci", 2, 3), p, 3, A.bitwise_and)
-    ts(V("ci", 3, 4), p, 4, A.arith_shift_right)
-    ts(V("ci", 4, 5), p, 1, A.arith_shift_right, 7, A.bitwise_and)
-    ts(V("ci", 5, 6), p, 1, A.bitwise_and)
     memset(V("cs1", 0, 2), -H * UNIT)
     memset(V("cs2", 0, 2), 0.0)
-    copy(V("cf", 0, 6), V("ci", 0, 6))
-    for b in range(4):
-        quant(*E(b), V("eye", 3 - b, 515 - b))
+    ts(V("ci", 0, 1), p, 15, A.bitwise_and)
+    ts(V("ci", 1, 2), p, 1, A.arith_shift_right, 7, A.bitwise_and)
+    ts(V("ci", 2, 3), p, 1, A.bitwise_and)
+    ts(V("ci", 3, 4), p, 4, A.arith_shift_right)
     copy(V("uo"), V("c16", 0, 8))
-    ts(col(FIRST), col(I16), 0.0, A.is_equal, 16.0, A.mult)
-    ts(col(LAST), col(I16), 15.0, A.is_equal, KEEP, A.mult)
-    ts(col(16), col(I4), 3.0, A.not_equal, -4 * KEEP, A.mult)
     memset(V("d1"), LOW)
     memset(V("ml0"), LOW)
+    copy(V("cf", 0, 3), V("ci", 0, 3))
     memset(V("ms1"), LOW)
-    act(V("cf", START16, START4 + 1), V("cf", I16, I4 + 1), 1.0, bias=2.0)
+    memset(V("d1", 2, 80, 4), 0.0)
+    ts(col(FIRST), col(I16), 0.0, A.is_equal, 16.0, A.mult)
+    ts(col(LAST), col(I16), 15.0, A.is_equal, KEEP, A.mult)
+    ts(col(16), col(I8), 7.0, A.not_equal, -KEEP, A.mult)
+    for b in range(4):
+        quant(*E(b), V("eye", 3 - b, 515 - b))
+    act(V("cf", START16, START8 + 1), V("cf", I16, I8 + 1), 1.0, bias=2.0)
+    act(col(I20), col(I16), 20.0)
     act(col(J1), col(FIRST), 2.0, bias=col(I16))
-    act(col(NOFF), col(16), 1.0, bias=col(T4))
+    act(col(NOFF), col(T2), float(NM), bias=col(16))
     act(col(P20), col(LAST), 20.0, bias=20 * (H - KEEP) + WHOLE * (C - 1))
     act(col(P16), col(LAST), 1.0, bias=H - KEEP - 7.5 + 16 * WHOLE)
-    ts(V("mk"), V("t16"), col(I16), A.is_equal, 16 * UNIT, A.mult)
     gi = V("ci", 3, 4)
-    op("gp", lambda: g.indirect_dma_start(T.lr0[:], None, T.stage[:], IndirectOffsetOnAxis(ap=ap(gi), axis=0), bounds_check=7),
-       [V("stage"), gi], [V("lr0")], dma=True)
+
+    def repeat(o, src):
+        op("gp", lambda: g.indirect_dma_start(T[o][:], None, T[src][:], IndirectOffsetOnAxis(ap=ap(gi), axis=0), bounds_check=7),
+           [V(src), gi], [V(o)], dma=True)
+
+    hop = _helpers(T, topo, core)
+    far = len(topo.engines(hop[0], T.cores[(rank + DIST[0]) % n]))
+    repeat("lr0", "stage")
+    iota(V("val1"), [[1, C]], -H, 0)
+    iota(V("t8"), [[0, H // 8], [1, 8]], 0, 0)
+    spread([V("out4", s, s + 1) for s in range(NH)], V("hi"), hop, "h0")
+    arrives(V("in4", 0, NH), "ai1", NH * far)
+    dma("sy", T.stage1[:, 0:C], T.in4[0:2], [V("in4", 0, 2)], [V("stage1", 0, C)])
+    dma("sy", T.stage1[:, C:2 * C], T.in4[2:4], [V("in4", 2, 4)], [V("stage1", C, 2 * C)])
     iota(V("val2"), [[C, 2], [1, H]], -240, 0)
 
     quant(V("uc0"), V("us0"), V("ut"))
+    ts(V("d1", 0, 80, 4), V("c16"), col(J1), A.add, -float(H), A.add)
+    memset(V("ms1", 2, 40, 4), 0.0)
     pick_codes(V("uc1"), V("uc0"), V("uo"))
     act(V("us1"), V("us0"), off=V("uo"))
     hold_pattern(V("h16"), V("t16", 0, H), col(START16))
-    hold_pattern(V("h4"), V("t4"), col(START4))
-    memset(V("d1", 2, 80, 4), 0.0)
-    memset(V("ms1", 2, 40, 4), 0.0)
-    ts(V("d1", 0, 80, 4), V("c16"), col(J1), A.add, -float(H), A.add)
-    quant(V("xc"), V("xs"), V("xt"))
-    mm(4, V("uc1"), V("us1"), V("xc"), V("xs"))
+    for s in range(2):
+        quant(V("xc", H * s, H * s + H), V("xs", H * s, H * s + H), V("xt", 4 * H * s, 4 * H * s + 4 * H))
+        mm(4 + s, V("uc1"), V("us1"), V("xc", H * s, H * s + H), V("xs", H * s, H * s + H))
+    ts(V("mk"), V("t16"), col(I16), A.is_equal, 16 * UNIT, A.mult)
     for b in range(4):
         mm(b, *E(b), V("xc"), V("xs"))
     for b in range(4):
         act(V("ff", C * b, C * b + C), bank(b, C), 0.5)
-    memset(V("pa"), 0.0)
-    memset(V("pb"), 1.0 - C)
 
-    def counts(w, cs, init, total):
-        ts(V("fl", 0, w), bank(4, w), 0.0, A.is_gt, UNIT / 2, A.mult)
+    def counts(w, cs, init, total, between):
+        for s in range(w // H):
+            ts(V("fl", H * s, H * s + H), bank(4 + s, H), 0.0, A.is_gt, UNIT / 2, A.mult)
+        between(0)
         scan(V(cs, 2, w + 2), V("fl", 0, w), V("fl", 0, w), init, A.add, A.add)
+        between(1)
         scan(V("hd", w, 2 * w), V(cs, 1, w + 1), V("mk", 1, w + 1), 1e6, A.min, A.add)
         total(V(cs, w + 1, w + 2))
         scan(V("hd", 0, w), V(cs, 2, w + 2), V("mk", 1, w + 1), 1e6, A.min, A.add)
 
-    counts(C, "cs1", -H * UNIT, lambda t: ts(V("tc", 0, 1), t, 1 / UNIT, A.mult))
+    def first_lists(step):
+        if step == 0:
+            ts(V("ro"), V("c16"), 1.0 / 16, A.mult, col(I20), A.add)
+            memset(V("pa"), 0.0)
+        else:
+            memset(V("pb"), 1.0 - C)
+
+    counts(C, "cs1", -H * UNIT, lambda t: ts(V("tc", 0, 1), t, 1 / UNIT, A.mult), first_lists)
+    hold_pattern(V("h8"), V("t8"), col(START8))
     he = V("hd", C + 15, 2 * C, 16)
     ts(V("ml0", 1, 80, 4), he, -2 / UNIT, A.mult, V("tc", 0, 1), A.add)
     ts(V("ml0", 3, 80, 4), he, 1 / UNIT, A.mult)
     tt(V("ml0", 2, 80, 4), he, V("hd", 15, C, 16), A.subtract)
 
-    hop = _helpers(T, topo, core)
     for k in range(1, len(DIST) + 1):
         end = k == len(DIST)
         to, frm = T.cores[(rank + DIST[k - 1]) % n], T.cores[(rank - DIST[k - 1]) % n]
@@ -355,7 +377,7 @@ def rank_program(g, core, T, topo):
         ab, nab, qc, qs = "ab%d" % (k - 1), "ab%d" % k, "sc%d" % k, "ss%d" % k
         if k == 1:
             fwin = [V("ff", C * b, C * b + C) for b in range(4)]
-            awin, bwin, vals, back = V("lr0", 0, C), V("lr0", C, 2 * C), V("val1"), float(H)
+            awin, bwin, vals, back = V(ab, 0, C), V(ab, C, 2 * C), V("val1"), float(H)
         else:
             fwin = [V("ff", s, s + 3 * H) for s in (0, H, 4 * H, 5 * H)]
             awin, bwin, vals, back = V(ab, 0, 3 * H), V(ab, H, 4 * H), V("val2"), 240.0
@@ -365,16 +387,15 @@ def rank_program(g, core, T, topo):
         ts(V("pos"), V("pf", 3, 80, 4), col(FIRST), A.subtract, float(H) if k == 1 else 0.0, A.add)
         if k == 1:
             for b in range(4):
-                mm((5, 6, 7, 4)[b], *E(b), V("mc"), V("ms"))
-            for b in range(4):
-                act(V("mh", b, 4 * NM, 4), bank((5, 6, 7, 4)[b], NM), 0.5)
+                mm(4 + b, *E(b), V("mc"), V("ms"))
+            act(V(ab, C, 2 * C), V("lr0", C, 2 * C), 16.0, off=V("ro"))
+            act(V(ab, 0, C), V("lr0", 0, C), off=V("ro"))
         op("ve", lambda: g.vector.tensor_copy(gat(V("oo"), V("pos")), ap(vals)), [vals, V("pos")], [V("oo")])
         for s in range(2):
             scan(V("ee", H * s, H * s + H), V("h16"), V("oo", s, C, 2), 0.0, A.add, A.max)
-        held = V("ee", 15, C, 16)
-        ts(V("off"), held, col(LAST), A.add, back - KEEP, A.add)
         lo, ho = V("off", 0, 10), V("off", 10, 20)
-        li, hi = (V("poff", 0, 10), V("poff", 10, 20)) if k == 1 else (lo, ho)
+        ts(lo, V("ee", 15, H, 16), col(LAST), A.add, back - KEEP, A.add)
+        ts(ho, V("ee", H + 15, C, 16), col(LAST), A.add, back - KEEP, A.add)
 
         def left(b):
             act(V("ll", H * b, H * b + H), fwin[b], off=lo)
@@ -384,59 +405,47 @@ def rank_program(g, core, T, topo):
 
         def middle(step):
             if step == 0:
-                tt(V("nn"), awin, V("nb"), A.add, off=hi)
+                tt(V("nn"), awin, V("nb"), A.add, off=ho)
             elif step == 1:
-                scan(V("n2"), V("h4"), V("nn"), 0.0, A.add, A.max)
+                scan(V("n2"), V("h8"), V("nn"), 0.0, A.add, A.max)
             else:
-                ts(V("noff"), V("n2", 3, H, 4), 4.0, A.mult, col(NOFF), A.add)
+                ts(V("noff"), V("n2", 7, H, 8), col(NOFF), A.add)
 
-        def indices():
-            act(V(nab, 0, H), awin, off=li)
-            act(V(nab, H, C), bwin, 16.0 if k == 1 else None, off=hi)
-
+        ts(V("nb"), bwin, NI / 16, A.mult, off=lo)
+        for b in PLANES:
+            left(b)
         if k == 1:
-            ts(V("pa", 1, 40, 2), held, col(P16), A.add, 1.0 / 16, A.mult)
-            ts(V("pb", 1, 40, 2), held, 20.0, A.mult, col(P20), A.add)
-            left(0)
-            left(1)
-            scan(V("pc"), V("pa"), V("pb"), 0.0, A.mult, A.add)
-            copy(V("poff"), V("pc", 1, 40, 2))
-            larger(0)
-            left(2)
-            act(V("nb"), bwin, float(NI), off=li)
-            left(3)
-            larger(1)
-            larger(2)
-            middle(0)
-            larger(3)
-            middle(1)
-            middle(2)
-        else:
-            ts(V("nb"), bwin, NI / 16, A.mult, off=li)
-            for b in range(4):
-                left(b)
-            for b in range(4):
-                if b < 3:
-                    middle(b)
-                larger(b)
-        indices()
+            for s, b in enumerate(PLANES):
+                act(V("mh", NM * s, NM * s + NM), bank(4 + b, NM), 0.5)
+        for s, b in enumerate(PLANES):
+            larger(b)
+            if s < 3:
+                middle(s)
+        act(V(nab, 0, H), awin, off=lo)
+        act(V(nab, H, C), bwin, off=ho)
         act(V("p32"), V("ph"), 64.0)
         far = len(topo.engines(hop[0] if k == 1 else core, to))
-        if k == 1:
-            spread([V(nab, PIECE * s, PIECE * s + PIECE) for s in range(NH)], V("hi"), hop, "h0")
-            arrives(V(nab, C, 2 * C), "ai1", NH * far)
+        if 1 < k < len(DIST):
+            send(V(nab, 0, C), V(nab, C, 2 * C), to, "ai%d" % k, topo.engines(core, to))
+            arrives(V(nab, C, 2 * C), "ai%d" % k, far)
         elif end:
             dma("sy", T.fold[:], T[nab][0:128:16, :], [V(nab)], [V("fold")])
             dma("sy", T.tb[0:8, 0:C], T[nab][0:128:16, :], [V(nab)], [V("tb", 0, C)])
             send(V("fold"), V("land"), to, "ai%d" % k, topo.engines(core, to))
             arrives(V("land"), "ai%d" % k, far)
             dma("sy", T.tb[0:8, C:2 * C], T.land[:], [V("land")], [V("tb", C, 2 * C)])
-        tt(V("zt"), V("mh"), V("ph"), A.add, off=V("noff"))
+        for s in range(2):
+            tt(V("zt", s, 4 * H, 2), V("mh", 2 * NM * s, 2 * NM * s + 2 * NM), V("ph", s, 4 * H, 2), A.add, off=V("noff"))
+        held = V("ee", 15, C, 16)
+        if k == 1:
+            ts(V("pa", 1, 40, 2), held, col(P16), A.add, 1.0 / 16, A.mult)
+            ts(V("pb", 1, 40, 2), held, 20.0, A.mult, col(P20), A.add)
         quant(V("zc"), V("zs"), V("zt"))
-        if 1 < k < len(DIST):
-            tt(V("pk"), V(nab, 0, H), V(nab, H, C), A.add)
-            send(V("pk"), V("pr"), to, "ai%d" % k, topo.engines(core, to))
-            arrives(V("pr"), "ai%d" % k, far)
+        if k == 1:
+            scan(V("pc"), V("pa"), V("pb"), 0.0, A.mult, A.add)
+            copy(V("poff"), V("pc", 1, 40, 2))
+            send(V("poff"), V("ho"), hop[SCALES], "h3", topo.engines(core, hop[SCALES]))
+            arrives(V("poff1"), "ao", far)
         for b in range(4):
             mm(b, V("wq", 128 * b, 128 * b + 128), V("wp", 128 * b, 128 * b + 128), V("zc"), V("zs"))
         for b in range(4):
@@ -464,13 +473,25 @@ def rank_program(g, core, T, topo):
         mm(4, V("uc1"), V("us1"), oc, os_)
         for b in range(4):
             mm(b, *E(b), oc, os_)
-        counts(H, "cs2", 0.0, lambda t: act(V("tc", 1, 2), t, 1 / UNIT))
+
+        def later_lists(step):
+            if k == 1 and step == 0:
+                ts(col(17), col(FIRST), 1.5, A.mult, col(I16), A.add)
+                memset(V("ms2"), LOW)
+                ts(col(18), col(T2), -float(H), A.mult, float(H), A.add)
+            elif k == 1:
+                ts(V("j2", 10, 20), V("c16", 0, 10), col(17), A.add, 2.0, A.mult)
+                memset(V("ms2", 2, 40, 4), 0.0)
+                tt(col(FO), col(18), col(I8), A.add)
+
+        counts(H, "cs2", 0.0, lambda t: act(V("tc", 1, 2), t, 1 / UNIT), later_lists)
         hb = V("hd", 15, 2 * H, 16)
         act(V(ms, 1, 80, 4), hb, -2 / UNIT, bias=V("tc", 1, 2))
         ts(V(ms, 3, 80, 4), hb, 1 / UNIT, A.mult)
         tt(V(ms, 42, 80, 4), V("hd", H + 15, 2 * H, 16), V("hd", 15, H, 16), A.subtract)
         if k == 1:
             send(V(ms), V("ht"), hop[LIST], "h1", topo.engines(core, hop[LIST]))
+            repeat("lr1", "stage1")
         else:
             send(V(ms), V(ml), to, "at%d" % k, topo.engines(core, to))
         arrives(V(ml), "at%d" % k, far)
@@ -478,10 +499,6 @@ def rank_program(g, core, T, topo):
         for b in range(4):
             act(V("ff", at[b], at[b] + H), bank(b, H), 0.5)
         if k == 1:
-            ts(col(17), col(FIRST), 1.5, A.mult, col(I16), A.add)
-            memset(V("ms2"), LOW)
-            ts(V("j2", 10, 20), V("c16", 0, 10), col(17), A.add, 2.0, A.mult)
-            memset(V("ms2", 2, 40, 4), 0.0)
             ts(V("j2", 0, 10), V("j2", 10, 20), 1.0, A.add)
         tt(V("tq", 0, 10), V(ms, 41, 80, 4), V(ms, 43, 80, 4), A.add)
         for s in range(2):
@@ -489,19 +506,16 @@ def rank_program(g, core, T, topo):
         tt(V("d1", 40, 80, 4), V("tq", 0, 10), V("j2", 10, 20), A.add)
         tt(V("tq", 10, 20), V("tq", 0, 10), V("j2", 0, 10), A.add)
         tt(V("d1", 0, 40, 4), V("tq", 10, 20), V(ms, 42, 80, 4), A.add)
-        if k > 1:
-            ts(V("pq"), V("pr"), 2304.0 - NI / 2, A.add)
-            ts(V(nab, 3 * H, 4 * H), V("pq"), -2304.0, A.add)
-            tt(V(nab, 2 * H, 3 * H), V("pr"), V(nab, 3 * H, 4 * H), A.subtract)
         if k == 1:
-            ts(col(18), col(5), -float(H), A.mult, float(H), A.add)
             quant(V("vc"), V("vs"), V("vt"))
-            tt(col(FO), col(18), col(4), A.add)
             ts(V("fo"), V("c16"), 0.5, A.mult, col(FO), A.add)
         for b in range(4):
             mm(4 + b, *E(b), rc, rs)
         for b in range(4):
             act(V("ff", at[b] + 2 * H, at[b] + 3 * H), bank(4 + b, H), 0.5)
+        if k == 1:
+            act(V(nab, 3 * H, 4 * H), V("lr1", C, 2 * C), 16.0, off=V("poff1", 10, 20))
+            act(V(nab, 2 * H, 3 * H), V("lr1", 0, C), off=V("poff1", 0, 10))
 
     mm(4, V("vc"), V("vs"), oc, os_)
     act(V("yy", 1, C, 2), bank(4, H))

@@ -10,6 +10,11 @@ LOW = -65536.0
 KEEP = 512.0
 WHOLE = 130.0
 NH = 4
+RUNS = ((64, H), (0, 64))
+PAD = 128 - RUNS[1][1]
+OWN = H + PAD
+UNPACK = ((1, 2, 3, 5), (6, 7, 0, 4))
+PICKED = ((1, 0), (1, 1))
 PLANES = (0, 2, 1, 3)
 
 
@@ -24,30 +29,31 @@ SCRATCH = {
     "mc": _sb(NM, X4), "ms": _sb(NM, U8), "vc": _sb(128, X4), "vs": _sb(128, U8), "wq": _sb(512, X4), "wp": _sb(512, U8),
     "eye": _sb(520, BF), "ec": _sb(512, X4), "es": _sb(512, U8),
     "pp": _sb(2, I32), "ci": _sb(8, I32), "cf": _sb(20, F32), "c16": _sb(20, F32),
-    "t16": _sb(336, BF), "t8": _sb(H, BF), "mk": _sb(336, BF), "h16": _sb(H, BF), "h8": _sb(H, BF), "ha": _sb(H, BF), "hb": _sb(H, BF),
+    "t16": _sb(H + 16, BF), "t8": _sb(H, BF), "mk": _sb(H + 16, BF), "h16": _sb(H, BF), "ha": _sb(H, BF), "hb": _sb(H, BF),
     "val1": _sb(C, BF), "val2": _sb(C, BF), "j2": _sb(20, F32),
     "uo": _sb(8, U16), "fo": _sb(20, U16),
     "stage": ("dram", [8, 2 * C], I32), "lr0": _sb(2 * C, I32),
     "ff": _sb(4 * C, BF), "mh": _sb(4 * NM, BF),
-    "fl": _sb(C, BF), "cs1": _sb(C + 2, BF), "cs2": _sb(H + 2, BF), "hd": _sb(2 * C, BF), "tc": _sb(2, F32),
+    "fl": _sb(C, BF), "cs1": _sb(H + 2, BF), "cs2": _sb(H + 2, BF), "hd": _sb(2 * C, BF), "tc": _sb(4, F32),
     "ml0": _sb(80, F32), "d1": _sb(80, F32), "pf": _sb(80, F32), "tq": _sb(20, F32),
     "pos": _sb(20, U16), "oo": _sb(C, BF), "ee": _sb(C, F16), "off": _sb(20, U16),
     "pa": _sb(40, BF), "pb": _sb(40, F32), "pc": _sb(40, F32), "poff": _sb(20, U16),
-    "nb": _sb(H, BF), "nn": _sb(H, BF), "n2": _sb(H, F16), "noff": _sb(20, U16), "ro": _sb(20, U16), "ab0": _sb(2 * C, BF),
-    "ll": _sb(4 * H, BF), "ph": _sb(4 * H, BF), "p32": _sb(4 * H, BF), "zt": _sb(4 * H, BF), "zc": _sb(H, X4), "zs": _sb(H, U8),
-    "v32": _sb(4 * H, BF), "vv": _sb(4 * H, BF),
+    "na": _sb(C, BF), "nb": _sb(C, BF), "n2": _sb(C, BF), "qa": _sb(H, BF), "qb": _sb(H, BF), "noff": _sb(20, U16), "ro": _sb(20, U16), "ab0": _sb(2 * C, BF),
+    "rr": _sb(H, BF), "mg": _sb(4 * H, BF), "ll": _sb(4 * H, BF), "ph": _sb(4 * H, BF), "p32": _sb(4 * H, BF), "zt": _sb(1024, BF), "zc": _sb(256, X4), "zs": _sb(256, U8),
+    "v32": _sb(4 * H, BF), "vv": _sb(1024, BF),
     "ab1": _sb(2 * C, BF), "ab2": _sb(2 * C, BF), "ab3": _sb(C, BF),
-    "sc1": _sb(C, X4), "sc2": _sb(C, X4), "sc3": _sb(C, X4), "ss1": _sb(C, U8), "ss2": _sb(C, U8), "ss3": _sb(C, U8),
+    "sc1": _sb(H + 256, X4), "sc2": _sb(H + 256, X4), "sc3": _sb(H + 256, X4),
+    "ss1": _sb(H + 256, U8), "ss2": _sb(H + 256, U8), "ss3": _sb(H + 256, U8),
     "ms1": _sb(80, BF), "ms2": _sb(80, BF), "ml1": _sb(80, BF), "ml2": _sb(80, BF),
     "out4": ("dram", [NH, 128, 10], I32), "hi": ("dram", [128, 10], I32), "in4": ("dram", [NH, 128, 10], I32),
     "stage1": ("dram", [8, 2 * C], I32), "lr1": _sb(2 * C, I32), "ho": _sb(20, U16), "poff1": _sb(20, U16),
     "fold": ("dram", [128, 20], BF), "land": ("dram", [128, 20], BF), "tb": _sb(2 * C, BF), "lro": _sb(2 * C, F32),
     "pkc": _sb(C, X4), "pks": _sb(C, U8), "yy": _sb(C, F32),
-    "hs1": _sb(H, U8), "hs2": _sb(H, U8), "hc": _sb(H // 2, X4), "ht": _sb(80, BF),
+    "hs1": _sb(H, U8), "hs2": _sb(H, U8), "hc": _sb(H, X4), "hc2": _sb(H, X4), "ht": _sb(80, BF),
 }
-NDMA = 28
+NDMA = 32
 SEMAPHORES = (["pe", "ve", "ac", "gp", "sent", "h0", "h1", "h2", "h3", "ao"] + ["d%d" % k for k in range(NDMA)]
-              + [a + str(k) for a in ("ai", "as", "at", "aq") for k in (1, 2, 3)])
+              + [a + str(k) for a in ("ai", "as", "at", "aq", "ar") for k in (1, 2, 3)])
 LIST, CODES_A, CODES_B, SCALES = range(NH)
 
 
@@ -88,13 +94,16 @@ def helper_program(g, core, T, topo):
         if role == LIST:
             jobs.append(("h1", full, ("ht", 0, 80), ("ml1", 0, 80), "at1", one))
         elif role == SCALES:
+            jobs.append(("h1", full, ("hs1", 0, H), ("ss1", 0, H), "as1", one))
             jobs.append(("h3", full, ("ho", 0, 20), ("poff1", 0, 20), "ao", one))
-            jobs.append(("h1", full, ("hs1", 0, H), ("ss1", H, C), "as1", one))
         else:
-            lo = H + (H // 2) * (role - CODES_A)
-            jobs.append(("h1", full // 2, ("hc", 0, H // 2), ("sc1", lo, lo + H // 2), "aq1", one))
+            lo, hi = RUNS[role - CODES_A]
+            jobs.append(("h1", full, ("hc", 0, hi - lo), ("sc1", lo, hi), ("aq1", "ar1")[role - CODES_A], one))
+        if role == LIST:
+            lo, hi = RUNS[0]
+            jobs.append(("h2", len(_spare(topo, src, core, two)), ("hc2", 0, hi - lo), ("sc2", lo, hi), "aq2", two))
         if role == CODES_A:
-            jobs.append(("h2", len(_spare(topo, src, core, two)), ("hs2", 0, H), ("ss2", H, C), "as2", two))
+            jobs.append(("h2", len(_spare(topo, src, core, two)), ("hs2", 0, H), ("ss2", 0, H), "as2", two))
         sent = 0
         for sem, val, a, b, far, dst in jobs:
             rid, pid = topo.addr(dst, core)
@@ -221,6 +230,13 @@ def rank_program(g, core, T, topo):
     def bank(b, w):
         return V("ps", 512 * b, 512 * b + w)
 
+    def window(r):
+        return 128 * (1 - r)
+
+    def valid(b, r):
+        lo_, hi_ = RUNS[r]
+        return V("ps", 512 * b + PAD + lo_ - window(r), 512 * b + PAD + hi_ - window(r))
+
     def mm(b, lc, ls, rc, rs):
         o = bank(b, rc[2] - rc[1])
         op("pe", lambda: g.tensor.matmul_mx(ap(o), ap(lc), ap(ls), ap(rc), ap(rs), True, True), [lc, ls, rc, rs], [o])
@@ -266,9 +282,9 @@ def rank_program(g, core, T, topo):
         return V("ec", 128 * b, 128 * b + 128), V("es", 128 * b, 128 * b + 128)
 
     def hold_pattern(o, t, start):
-        act(V("ha"), t, -1.0, bias=start, func=ACT.Relu)
-        act(V("hb"), V("ha"), 1.0, bias=-0.75, func=ACT.Square)
-        act(o, V("hb"), -2 * KEEP, bias=2 * KEEP * 0.5625)
+        yield act(V("ha"), t, -1.0, bias=start, func=ACT.Relu)
+        yield act(V("hb"), V("ha"), 1.0, bias=-0.75, func=ACT.Square)
+        yield act(o, V("hb"), -2 * KEEP, bias=2 * KEEP * 0.5625)
 
     dma("ac", T.stage[:, 0:C], T.li[:], [], [V("stage", 0, C)])
     dma("sy", T.stage[:, C:2 * C], T.ri[:], [], [V("stage", C, 2 * C)])
@@ -283,15 +299,15 @@ def rank_program(g, core, T, topo):
     dma("sy", T.wp[:], T.ws[:], [], [V("wp")])
     dma("sy", T.vt[:], T.v[:], [], [V("vt")])
 
-    I16, I8, T2, I20, FIRST, LAST, J1, START16, START8, NOFF, P20, P16, FO = 0, 1, 2, 5, 6, 7, 8, 9, 10, 11, 12, 13, 15
+    I16, I8, T2, I20, FIRST, LAST, J1, START16, NOFF, P20, P16, FO = 0, 1, 2, 5, 6, 7, 8, 9, 11, 12, 13, 15
     memset(V("eye"), 0.0)
     iota(V("pp"), [[0, 2]], 0, 1)
     iota(V("c16"), [[16, 20]], 0, 0)
     diag = V("eye", 3, 515, 4)
     op("gp", lambda: g.affine_select(ap(diag), ap(diag), [[1, 128]], A.not_equal, 1.0, 0, -1), [diag], [diag])
-    iota(V("t16"), [[0, 21], [1, 16]], 0, 0)
+    iota(V("t16"), [[0, H // 16 + 1], [1, 16]], 0, 0)
     p = V("pp", 0, 1)
-    memset(V("cs1", 0, 2), -H * UNIT)
+    memset(V("cs1", 0, 2), 0.0)
     memset(V("cs2", 0, 2), 0.0)
     ts(V("ci", 0, 1), p, 15, A.bitwise_and)
     ts(V("ci", 1, 2), p, 1, A.arith_shift_right, 7, A.bitwise_and)
@@ -305,13 +321,12 @@ def rank_program(g, core, T, topo):
     memset(V("d1", 2, 80, 4), 0.0)
     ts(col(FIRST), col(I16), 0.0, A.is_equal, 16.0, A.mult)
     ts(col(LAST), col(I16), 15.0, A.is_equal, KEEP, A.mult)
-    ts(col(16), col(I8), 7.0, A.not_equal, -KEEP, A.mult)
     for b in range(4):
         quant(*E(b), V("eye", 3 - b, 515 - b))
-    act(V("cf", START16, START8 + 1), V("cf", I16, I8 + 1), 1.0, bias=2.0)
+    act(col(START16), col(I16), 1.0, bias=2.0)
     act(col(I20), col(I16), 20.0)
     act(col(J1), col(FIRST), 2.0, bias=col(I16))
-    act(col(NOFF), col(T2), float(NM), bias=col(16))
+    act(col(NOFF), col(T2), float(NM))
     act(col(P20), col(LAST), 20.0, bias=20 * (H - KEEP) + WHOLE * (C - 1))
     act(col(P16), col(LAST), 1.0, bias=H - KEEP - 7.5 + 16 * WHOLE)
     gi = V("ci", 3, 4)
@@ -332,43 +347,56 @@ def rank_program(g, core, T, topo):
     iota(V("val2"), [[C, 2], [1, H]], -240, 0)
 
     quant(V("uc0"), V("us0"), V("ut"))
-    ts(V("d1", 0, 80, 4), V("c16"), col(J1), A.add, -float(H), A.add)
+    ts(V("d1", 0, 80, 4), V("c16"), col(J1), A.add)
     memset(V("ms1", 2, 40, 4), 0.0)
+    memset(V("pa"), 0.0)
     pick_codes(V("uc1"), V("uc0"), V("uo"))
     act(V("us1"), V("us0"), off=V("uo"))
-    hold_pattern(V("h16"), V("t16", 0, H), col(START16))
+    memset(V("zt", 0, 4 * PAD), 0.0)
+    memset(V("zt", 4 * (PAD + H)), 0.0)
+    list(hold_pattern(V("h16"), V("t16", 0, H), col(START16)))
     for s in range(2):
         quant(V("xc", H * s, H * s + H), V("xs", H * s, H * s + H), V("xt", 4 * H * s, 4 * H * s + 4 * H))
         mm(4 + s, V("uc1"), V("us1"), V("xc", H * s, H * s + H), V("xs", H * s, H * s + H))
     ts(V("mk"), V("t16"), col(I16), A.is_equal, 16 * UNIT, A.mult)
+    memset(V("vv", 0, 4 * PAD), 0.0)
+    memset(V("vv", 4 * (PAD + H)), 0.0)
     for b in range(4):
         mm(b, *E(b), V("xc"), V("xs"))
-    for b in range(4):
+
+    def unpack_x(b):
         act(V("ff", C * b, C * b + C), bank(b, C), 0.5)
 
-    def counts(w, cs, init, total, between):
-        for s in range(w // H):
-            ts(V("fl", H * s, H * s + H), bank(4 + s, H), 0.0, A.is_gt, UNIT / 2, A.mult)
-        between(0)
-        scan(V(cs, 2, w + 2), V("fl", 0, w), V("fl", 0, w), init, A.add, A.add)
-        between(1)
-        scan(V("hd", w, 2 * w), V(cs, 1, w + 1), V("mk", 1, w + 1), 1e6, A.min, A.add)
-        total(V(cs, w + 1, w + 2))
-        scan(V("hd", 0, w), V(cs, 2, w + 2), V("mk", 1, w + 1), 1e6, A.min, A.add)
+    def flags(lo_, hi_, src):
+        ts(V("fl", lo_, hi_), src, 0.0, A.is_gt, UNIT / 2, A.mult)
 
-    def first_lists(step):
-        if step == 0:
-            ts(V("ro"), V("c16"), 1.0 / 16, A.mult, col(I20), A.add)
-            memset(V("pa"), 0.0)
-        else:
-            memset(V("pb"), 1.0 - C)
+    def running(cs, lo_):
+        scan(V(cs, 2, H + 2), V("fl", lo_, lo_ + H), V("fl", lo_, lo_ + H), 0.0, A.add, A.add)
 
-    counts(C, "cs1", -H * UNIT, lambda t: ts(V("tc", 0, 1), t, 1 / UNIT, A.mult), first_lists)
-    hold_pattern(V("h8"), V("t8"), col(START8))
-    he = V("hd", C + 15, 2 * C, 16)
-    ts(V("ml0", 1, 80, 4), he, -2 / UNIT, A.mult, V("tc", 0, 1), A.add)
-    ts(V("ml0", 3, 80, 4), he, 1 / UNIT, A.mult)
-    tt(V("ml0", 2, 80, 4), he, V("hd", 15, C, 16), A.subtract)
+    def held_counts(cs, at):
+        scan(V("hd", at + H, at + C), V(cs, 1, H + 1), V("mk", 1, H + 1), 1e6, A.min, A.add)
+        scan(V("hd", at, at + H), V(cs, 2, H + 2), V("mk", 1, H + 1), 1e6, A.min, A.add)
+        return V("hd", at + H + 15, at + C, 16), V("hd", at + 15, at + H, 16)
+
+    flags(0, H, bank(4, H))
+    flags(H, C, bank(5, H))
+    running("cs1", 0)
+    ts(V("ro"), V("c16"), 1.0 / 16, A.mult, col(I20), A.add)
+    running("cs2", H)
+    first, second = V("cs1", H + 1, H + 2), V("cs2", H + 1, H + 2)
+    unpack_x(0)
+    act(V("tc", 2, 3), first, 1 / UNIT)
+    act(V("tc", 1, 2), second, 1 / UNIT)
+    act(V("tc", 0, 1), second, 1 / UNIT, bias=V("tc", 2, 3))
+    counts = [held_counts("cs1", 0), held_counts("cs2", C)]
+    ts(V("d1", 42, 80, 4), V("d1", 2, 40, 4), V("tc", 2, 3), A.add)
+    for s in (1, 0):
+        act(V("ml0", 40 * s + 1, 40 * s + 40, 4), counts[s][0], -2 / UNIT, bias=V("tc", s, s + 1))
+    for s in range(2):
+        ts(V("ml0", 40 * s + 3, 40 * s + 40, 4), counts[s][0], 1 / UNIT, A.mult)
+        tt(V("ml0", 40 * s + 2, 40 * s + 40, 4), *counts[s], A.subtract)
+    for b in range(1, 4):
+        unpack_x(b)
 
     for k in range(1, len(DIST) + 1):
         end = k == len(DIST)
@@ -384,18 +412,31 @@ def rank_program(g, core, T, topo):
         scan(V("pf"), V("ml%d" % (k - 1)), V("d1"), 0.0, A.add, A.max)
         if k == 1:
             quant(V("mc"), V("ms"), V("mt"))
-        ts(V("pos"), V("pf", 3, 80, 4), col(FIRST), A.subtract, float(H) if k == 1 else 0.0, A.add)
+            ts(V("qa"), V("t8"), col(I8), A.is_equal, UNIT, A.mult)
+        ts(V("pos"), V("pf", 3, 80, 4), col(FIRST), A.subtract)
         if k == 1:
+            memset(V("pb"), 1.0 - C)
+            memset(V("nb", 1, C, 2), -UNIT)
+            act(V("qb"), V("qa"), 2.0, bias=-UNIT)
+            act(V("na", 0, C, 2), V("qa"), -1.0)
             for b in range(4):
                 mm(4 + b, *E(b), V("mc"), V("ms"))
-            act(V(ab, C, 2 * C), V("lr0", C, 2 * C), 16.0, off=V("ro"))
+            act(V(ab, C, 2 * C), V("lr0", C, 2 * C), float(NI), off=V("ro"))
             act(V(ab, 0, C), V("lr0", 0, C), off=V("ro"))
+
+        def unpack_mid(*planes):
+            for s in planes if k == 1 else ():
+                ts(V("mh", NM * s, NM * s + NM), bank(4 + PLANES[s], NM), 0.5, A.mult)
+
         op("ve", lambda: g.vector.tensor_copy(gat(V("oo"), V("pos")), ap(vals)), [vals, V("pos")], [V("oo")])
+        unpack_mid(0, 1)
         for s in range(2):
             scan(V("ee", H * s, H * s + H), V("h16"), V("oo", s, C, 2), 0.0, A.add, A.max)
+        unpack_mid(2)
         lo, ho = V("off", 0, 10), V("off", 10, 20)
         ts(lo, V("ee", 15, H, 16), col(LAST), A.add, back - KEEP, A.add)
         ts(ho, V("ee", H + 15, C, 16), col(LAST), A.add, back - KEEP, A.add)
+        unpack_mid(3)
 
         def left(b):
             act(V("ll", H * b, H * b + H), fwin[b], off=lo)
@@ -404,26 +445,26 @@ def rank_program(g, core, T, topo):
             tt(V("ph", b, 4 * H, 4), fwin[b], V("ll", H * b, H * b + H), A.max, off=ho)
 
         def middle(step):
-            if step == 0:
-                tt(V("nn"), awin, V("nb"), A.add, off=ho)
-            elif step == 1:
-                scan(V("n2"), V("h8"), V("nn"), 0.0, A.add, A.max)
+            if step == 1:
+                scan(V("n2"), V("na"), V("nb"), 0.0, A.add, A.max)
             else:
-                ts(V("noff"), V("n2", 7, H, 8), col(NOFF), A.add)
+                ts(V("noff"), V("n2", 15, C, 16), col(NOFF), A.add)
 
-        ts(V("nb"), bwin, NI / 16, A.mult, off=lo)
+        tt(V("nb", 0, C, 2), bwin, V("qb"), A.min, off=lo)
+        tt(V("na", 1, C, 2), awin, V("qa"), A.min, off=ho)
         for b in PLANES:
             left(b)
-        if k == 1:
-            for s, b in enumerate(PLANES):
-                act(V("mh", NM * s, NM * s + NM), bank(4 + b, NM), 0.5)
-        for s, b in enumerate(PLANES):
+        act(V("rr"), fwin[PLANES[3]], off=ho)
+        for s, b in enumerate(PLANES[:3]):
             larger(b)
-            if s < 3:
-                middle(s)
+            if s < 2:
+                middle(s + 1)
+        tt(V("ph", PLANES[3], 4 * H, 4), V("rr"), V("ll", H * PLANES[3], H * PLANES[3] + H), A.max)
         act(V(nab, 0, H), awin, off=lo)
+        for r, s in PICKED:
+            lo_, hi_ = RUNS[r]
+            act(V("mg", 4 * lo_ + s, 4 * hi_, 2), V("mh", 2 * NM * s, 2 * NM * s + 2 * NM), off=V("noff", lo_ // 8, hi_ // 8))
         act(V(nab, H, C), bwin, off=ho)
-        act(V("p32"), V("ph"), 64.0)
         far = len(topo.engines(hop[0] if k == 1 else core, to))
         if 1 < k < len(DIST):
             send(V(nab, 0, C), V(nab, C, 2 * C), to, "ai%d" % k, topo.engines(core, to))
@@ -434,70 +475,109 @@ def rank_program(g, core, T, topo):
             send(V("fold"), V("land"), to, "ai%d" % k, topo.engines(core, to))
             arrives(V("land"), "ai%d" % k, far)
             dma("sy", T.tb[0:8, C:2 * C], T.land[:], [V("land")], [V("tb", C, 2 * C)])
-        for s in range(2):
-            tt(V("zt", s, 4 * H, 2), V("mh", 2 * NM * s, 2 * NM * s + 2 * NM), V("ph", s, 4 * H, 2), A.add, off=V("noff"))
+        def middle_sum(r, s):
+            lo_, hi_ = RUNS[r]
+            o, p_ = V("zt", 4 * (PAD + lo_) + s, 4 * (PAD + hi_), 2), V("ph", 4 * lo_ + s, 4 * hi_, 2)
+            if (r, s) in PICKED:
+                tt(o, V("mg", 4 * lo_ + s, 4 * hi_, 2), p_, A.add)
+            else:
+                tt(o, V("mh", 2 * NM * s, 2 * NM * s + 2 * NM), p_, A.add, off=V("noff", lo_ // 8, hi_ // 8))
+
+        def larger32(r):
+            lo_, hi_ = RUNS[r]
+            ts(V("p32", 4 * lo_, 4 * hi_), V("ph", 4 * lo_, 4 * hi_), 64.0, A.mult)
+
+        def layer(r):
+            w = window(r)
+            quant(V("zc", w, w + 128), V("zs", w, w + 128), V("zt", 4 * w, 4 * w + 512))
+            for b in range(4):
+                mm(4 * r + b, V("wq", 128 * b, 128 * b + 128), V("wp", 128 * b, 128 * b + 128), V("zc", w, w + 128), V("zs", w, w + 128))
+
+        def add_larger(r):
+            lo_, hi_ = RUNS[r]
+            for b in range(4):
+                sums = V("v32", H * b + lo_, H * b + hi_)
+                tt(sums, valid(4 * r + b, r), V("p32", 4 * lo_ + b, 4 * hi_, 4), A.add)
+                act(V("vv", 4 * (PAD + lo_) + b, 4 * (PAD + hi_), 4), sums, 1.0 / 32)
+
+        def new_half(r):
+            w = window(r)
+            c, s = V(qc, H + w, H + w + 128), V(qs, H + w, H + w + 128)
+            quant(c, s, V("vv", 4 * w, 4 * w + 512))
+            mm(4 * r, *((V("vc"), V("vs")) if end else (V("uc1"), V("us1"))), c, s)
+
+        def send_codes(r):
+            lo_, hi_ = RUNS[r]
+            sem = ("aq%d", "ar%d")[r] % k
+            if k == 1:
+                send(V(qc, OWN + lo_, OWN + hi_), V("hc", 0, hi_ - lo_), hop[CODES_A + r], "h1", topo.engines(core, hop[CODES_A + r]))
+            elif not end and r == 0:
+                send(V(qc, OWN + lo_, OWN + hi_), V("hc2", 0, hi_ - lo_), hop[LIST], "h2", _spare(topo, core, hop[LIST], to))
+            else:
+                send(V(qc, OWN + lo_, OWN + hi_), V(qc, lo_, hi_), to, sem, topo.engines(core, to))
+            arrives(V(qc, lo_, hi_), sem, far)
+
+        oc, os_, rc, rs = V(qc, OWN, OWN + H), V(qs, OWN, OWN + H), V(qc, 0, H), V(qs, 0, H)
         held = V("ee", 15, C, 16)
+        middle_sum(0, 0)
+        middle_sum(0, 1)
+        middle_sum(1, 0)
+        middle_sum(1, 1)
+        layer(0)
+        larger32(0)
+        layer(1)
+        larger32(1)
+        add_larger(0)
+        add_larger(1)
         if k == 1:
             ts(V("pa", 1, 40, 2), held, col(P16), A.add, 1.0 / 16, A.mult)
             ts(V("pb", 1, 40, 2), held, 20.0, A.mult, col(P20), A.add)
-        quant(V("zc"), V("zs"), V("zt"))
+        new_half(0)
+        send_codes(0)
         if k == 1:
             scan(V("pc"), V("pa"), V("pb"), 0.0, A.mult, A.add)
-            copy(V("poff"), V("pc", 1, 40, 2))
-            send(V("poff"), V("ho"), hop[SCALES], "h3", topo.engines(core, hop[SCALES]))
-            arrives(V("poff1"), "ao", far)
-        for b in range(4):
-            mm(b, V("wq", 128 * b, 128 * b + 128), V("wp", 128 * b, 128 * b + 128), V("zc"), V("zs"))
-        for b in range(4):
-            tt(V("v32", H * b, H * b + H), bank(b, H), V("p32", b, 4 * H, 4), A.add)
-            if b < 3:
-                act(V("vv", b, 4 * H, 4), V("v32", H * b, H * b + H), 1.0 / 32)
-            else:
-                ts(V("vv", b, 4 * H, 4), V("v32", H * b, H * b + H), 1.0 / 32, A.mult)
-        oc, os_, rc, rs = V(qc, 0, H), V(qs, 0, H), V(qc, H, C), V(qs, H, C)
-        quant(oc, os_, V("vv"))
+        new_half(1)
+        if end:
+            send(os_, rs, to, "as%d" % k, topo.engines(core, to))
+        send_codes(1)
         if k == 1:
-            spread([V(qc, 0, H // 2), V(qc, H // 2, H)], V("hc"), [hop[CODES_A], hop[CODES_B]], "h1")
             send(os_, V("hs1"), hop[SCALES], "h1", topo.engines(core, hop[SCALES]))
-        else:
-            send(oc, rc, to, "aq%d" % k, topo.engines(core, to))
-            if end:
-                send(os_, rs, to, "as%d" % k, topo.engines(core, to))
-            else:
-                send(os_, V("hs2"), hop[CODES_A], "h2", _spare(topo, core, hop[CODES_A], to))
+            copy(V("poff"), V("pc", 1, 40, 2))
+        elif not end:
+            send(os_, V("hs2"), hop[CODES_A], "h2", _spare(topo, core, hop[CODES_A], to))
         arrives(rs, "as%d" % k, far)
-        arrives(rc, "aq%d" % k, 2 * far if k == 1 else far)
         if end:
             break
         ms, ml = "ms%d" % k, "ml%d" % k
-        mm(4, V("uc1"), V("us1"), oc, os_)
         for b in range(4):
-            mm(b, *E(b), oc, os_)
-
-        def later_lists(step):
-            if k == 1 and step == 0:
-                ts(col(17), col(FIRST), 1.5, A.mult, col(I16), A.add)
-                memset(V("ms2"), LOW)
-                ts(col(18), col(T2), -float(H), A.mult, float(H), A.add)
-            elif k == 1:
-                ts(V("j2", 10, 20), V("c16", 0, 10), col(17), A.add, 2.0, A.mult)
-                memset(V("ms2", 2, 40, 4), 0.0)
-                tt(col(FO), col(18), col(I8), A.add)
-
-        counts(H, "cs2", 0.0, lambda t: act(V("tc", 1, 2), t, 1 / UNIT), later_lists)
+            mm(UNPACK[0][b], *E(b), oc, os_)
+        for r in range(2):
+            flags(*RUNS[r], valid(4 * r, r))
+        if k == 1:
+            ts(col(17), col(FIRST), 1.5, A.mult, col(I16), A.add)
+            memset(V("ms2"), LOW)
+            ts(col(FO), col(T2), float(OWN), A.mult, col(I8), A.add)
+        running("cs2", 0)
+        if k == 1:
+            ts(V("j2", 10, 20), V("c16", 0, 10), col(17), A.add, 2.0, A.mult)
+            memset(V("ms2", 2, 40, 4), 0.0)
+        act(V("tc", 1, 2), second, 1 / UNIT)
+        without, with_ = held_counts("cs2", 0)
         hb = V("hd", 15, 2 * H, 16)
         act(V(ms, 1, 80, 4), hb, -2 / UNIT, bias=V("tc", 1, 2))
         ts(V(ms, 3, 80, 4), hb, 1 / UNIT, A.mult)
-        tt(V(ms, 42, 80, 4), V("hd", H + 15, 2 * H, 16), V("hd", 15, H, 16), A.subtract)
+        tt(V(ms, 42, 80, 4), without, with_, A.subtract)
         if k == 1:
             send(V(ms), V("ht"), hop[LIST], "h1", topo.engines(core, hop[LIST]))
+            send(V("poff"), V("ho"), hop[SCALES], "h3", topo.engines(core, hop[SCALES]))
+            arrives(V("poff1"), "ao", far)
             repeat("lr1", "stage1")
         else:
             send(V(ms), V(ml), to, "at%d" % k, topo.engines(core, to))
         arrives(V(ml), "at%d" % k, far)
         at = (0, H, 4 * H, 5 * H)
         for b in range(4):
-            act(V("ff", at[b], at[b] + H), bank(b, H), 0.5)
+            act(V("ff", at[b], at[b] + H), bank(UNPACK[0][b], H), 0.5)
         if k == 1:
             ts(V("j2", 0, 10), V("j2", 10, 20), 1.0, A.add)
         tt(V("tq", 0, 10), V(ms, 41, 80, 4), V(ms, 43, 80, 4), A.add)
@@ -508,30 +588,42 @@ def rank_program(g, core, T, topo):
         tt(V("d1", 0, 40, 4), V("tq", 10, 20), V(ms, 42, 80, 4), A.add)
         if k == 1:
             quant(V("vc"), V("vs"), V("vt"))
-            ts(V("fo"), V("c16"), 0.5, A.mult, col(FO), A.add)
+            ts(V("tq"), V("c16"), 0.5, A.mult, col(FO), A.add)
+            for lo_, hi_ in RUNS:
+                ts(V("fo", lo_ // 8, hi_ // 8), V("tq", lo_ // 8, hi_ // 8), -float(lo_), A.add)
         for b in range(4):
-            mm(4 + b, *E(b), rc, rs)
+            mm(UNPACK[1][b], *E(b), rc, rs)
         for b in range(4):
-            act(V("ff", at[b] + 2 * H, at[b] + 3 * H), bank(4 + b, H), 0.5)
+            act(V("ff", at[b] + 2 * H, at[b] + 3 * H), bank(UNPACK[1][b], H), 0.5)
         if k == 1:
-            act(V(nab, 3 * H, 4 * H), V("lr1", C, 2 * C), 16.0, off=V("poff1", 10, 20))
+            act(V(nab, 3 * H, 4 * H), V("lr1", C, 2 * C), float(NI), off=V("poff1", 10, 20))
             act(V(nab, 2 * H, 3 * H), V("lr1", 0, C), off=V("poff1", 0, 10))
 
-    mm(4, V("vc"), V("vs"), oc, os_)
-    act(V("yy", 1, C, 2), bank(4, H))
-    for s in range(2):
-        for lo, at in ((H * s, C * s + 1), (C + H * s, C * s)):
-            op("ve", lambda: g.vector.tensor_scalar(T.lro[0:8, at:C * s + C:2], T.tb[0:8, lo:lo + H], (1.0, 1.0 / 16)[s], None, A.mult),
+    for r, (lo_, hi_) in enumerate(RUNS):
+        act(V("yy", 2 * lo_ + 1, 2 * hi_, 2), valid(4 * r, r))
+
+    def last_indices(own):
+        for s in range(2):
+            lo, at = C * (1 - own) + H * s, C * s + own
+            op("ve", lambda: g.vector.tensor_scalar(T.lro[0:8, at:C * s + C:2], T.tb[0:8, lo:lo + H], (1.0, 1.0 / NI)[s], None, A.mult),
                [V("tb", lo, lo + H)], [V("lro", at, C * s + C, 2)])
+
+    last_indices(1)
+    for r, (lo_, hi_) in enumerate(RUNS):
+        a, b = 2 * lo_, 2 * hi_
+        pick_codes(V("pkc", a, b), V(qc, lo_), V("fo", lo_ // 8, hi_ // 8))
+        dma("sy", T.oc[:, 4 * a:4 * b], T.pkc[:, a:b].bitcast(dt.uint8), [V("pkc", a, b)], [])
+        mm(1 + r, V("vc"), V("vs"), V(qc, lo_, lo_ + 128), V(qs, lo_, lo_ + 128))
+        act(V("yy", a, b, 2), bank(1 + r, hi_ - lo_))
+        dma("ac", T.y[:, a:b], T.yy[:, a:b], [V("yy", a, b)], [])
+        if r == 0:
+            for lo2, hi2 in RUNS:
+                o, win, off = V("pks", 2 * lo2, 2 * hi2), V(qs, lo2), V("fo", lo2 // 8, hi2 // 8)
+                op("ve", lambda: g.vector.tensor_copy(ap(o), gat(win, off)), [win, off], [o])
+            for a in range(4):
+                dma("sy", T.osc[4 * a:4 * a + 4, 0:C], T.pks[32 * a:32 * a + 4, 0:C], [V("pks")], [])
+    last_indices(0)
     dma("sy", T.lr[:], T.lro[0:8, :], [V("lro")], [])
-    pick_codes(V("pkc"), V(qc), V("fo"))
-    dma("sy", T.oc[:], T.pkc[:].bitcast(dt.uint8), [V("pkc")], [])
-    mm(5, V("vc"), V("vs"), rc, rs)
-    act(V("yy", 0, C, 2), bank(5, H))
-    dma("ac", T.y[:], T.yy[:], [V("yy")], [])
-    op("ve", lambda: g.vector.tensor_copy(ap(V("pks")), gat(V(qs), V("fo"))), [V(qs), V("fo")], [V("pks")])
-    for a in range(4):
-        dma("sy", T.osc[4 * a:4 * a + 4, 0:C], T.pks[32 * a:32 * a + 4, 0:C], [V("pks")], [])
     last["sent"] = count["sent"]
     for s, val in last.items():
         if waited.get(s, 0) < val:

from concourse.bass import DstId, RemoteDMATransfer, IndirectOffsetOnAxis
from concourse.mybir import dt, AluOpType, ActivationFunctionType

C, H, NI = 320, 160, 12
NM = NI * NI
DIST = [1, 2, 4]
BF, F16, F32, I32, U16, U8, X4 = "bfloat16", "float16", "float32", "int32", "uint16", "uint8", "float8_e4m3fn_x4"
UNIT = 1024.0
LOW = -65536.0
KEEP = 512.0
WHOLE = 130.0
NH = 4
RUNS = ((64, H), (0, 64))
PAD = 128 - RUNS[1][1]
OWN = H + PAD
UNPACK = ((1, 2, 3, 5), (6, 7, 0, 4))
PICKED = ((1, 0), (1, 1))
PLANES = (0, 2, 1, 3)


def _sb(n, d):
    return ("sbuf", [128, n], d)


SCRATCH = {
    "ps": ("psum", [128, 4096], F32),
    "xt": _sb(4 * C, BF), "ut": _sb(512, BF), "mt": _sb(4 * NM, BF), "vt": _sb(512, BF),
    "xc": _sb(C, X4), "xs": _sb(C, U8), "uc0": _sb(128, X4), "us0": _sb(128, U8), "uc1": _sb(128, X4), "us1": _sb(128, U8),
    "mc": _sb(NM, X4), "ms": _sb(NM, U8), "vc": _sb(128, X4), "vs": _sb(128, U8), "wq": _sb(512, X4), "wp": _sb(512, U8),
    "eye": _sb(520, BF), "ec": _sb(512, X4), "es": _sb(512, U8),
    "pp": _sb(2, I32), "ci": _sb(8, I32), "cf": _sb(20, F32), "c16": _sb(20, F32),
    "t16": _sb(H + 16, BF), "t8": _sb(H, BF), "mk": _sb(H + 16, BF), "h16": _sb(H, BF), "ha": _sb(H, BF), "hb": _sb(H, BF),
    "val1": _sb(C, BF), "val2": _sb(C, BF), "j2": _sb(20, F32),
    "uo": _sb(8, U16), "fo": _sb(20, U16),
    "stage": ("dram", [8, 2 * C], I32), "lr0": _sb(2 * C, I32),
    "ff": _sb(4 * C, BF), "mh": _sb(4 * NM, BF),
    "fl": _sb(C, BF), "cs1": _sb(H + 2, BF), "cs2": _sb(H + 2, BF), "hd": _sb(2 * C, BF), "tc": _sb(4, F32),
    "ml0": _sb(80, F32), "d1": _sb(80, F32), "pf": _sb(80, F32), "tq": _sb(20, F32),
    "pos": _sb(20, U16), "oo": _sb(C, BF), "ee": _sb(C, F16), "off": _sb(20, U16),
    "pa": _sb(40, BF), "pb": _sb(40, F32), "pc": _sb(40, F32), "poff": _sb(20, U16),
    "na": _sb(C, BF), "nb": _sb(C, BF), "n2": _sb(C, BF), "qa": _sb(H, BF), "qb": _sb(H, BF), "noff": _sb(20, U16), "ro": _sb(20, U16), "ab0": _sb(2 * C, BF),
    "rr": _sb(H, BF), "mg": _sb(4 * H, BF), "ll": _sb(4 * H, BF), "ph": _sb(4 * H, BF), "p32": _sb(4 * H, BF), "zt": _sb(1024, BF), "zc": _sb(256, X4), "zs": _sb(256, U8),
    "v32": _sb(4 * H, BF), "vv": _sb(1024, BF),
    "ab1": _sb(2 * C, BF), "ab2": _sb(2 * C, BF), "ab3": _sb(C, BF),
    "sc1": _sb(H + 256, X4), "sc2": _sb(H + 256, X4), "sc3": _sb(H + 256, X4),
    "ss1": _sb(H + 256, U8), "ss2": _sb(H + 256, U8), "ss3": _sb(H + 256, U8),
    "ms1": _sb(80, BF), "ms2": _sb(80, BF), "ml1": _sb(80, BF), "ml2": _sb(80, BF),
    "out4": ("dram", [NH, 128, 10], I32), "hi": ("dram", [128, 10], I32), "in4": ("dram", [NH, 128, 10], I32),
    "stage1": ("dram", [8, 2 * C], I32), "lr1": _sb(2 * C, I32), "ho": _sb(20, U16), "poff1": _sb(20, U16),
    "fold": ("dram", [128, 20], BF), "land": ("dram", [128, 20], BF), "tb": _sb(2 * C, BF), "lro": _sb(2 * C, F32),
    "pkc": _sb(C, X4), "pks": _sb(C, U8), "yy": _sb(C, F32),
    "hs1": _sb(H, U8), "hs2": _sb(H, U8), "hc": _sb(H, X4), "hc2": _sb(H, X4), "ht": _sb(80, BF),
}
NDMA = 32
SEMAPHORES = (["pe", "ve", "ac", "gp", "sent", "h0", "h1", "h2", "h3", "ao"] + ["d%d" % k for k in range(NDMA)]
              + [a + str(k) for a in ("ai", "as", "at", "aq", "ar") for k in (1, 2, 3)])
LIST, CODES_A, CODES_B, SCALES = range(NH)


def _bits(engines):
    m = 0
    for e in engines:
        m |= 1 << e
    return m


def _helpers(T, topo, src):
    dst = T.cores[(T.rank_of(src) + DIST[0]) % len(T.cores)]
    h = [c for c in topo.cores_of(src) if T.rank_of(c) is None and topo.may_write(c, dst)]
    h.sort(key=lambda c: topo.die(c) != topo.die(src))
    return h[:NH]


def _spare(topo, src, near, far):
    return [e for e in topo.engines(src, near) if e not in topo.engines(src, far)]


def _raw(T, name, lo, hi):
    where, shape, _ = SCRATCH[name]
    a = T[name][:, lo:hi] if where == "sbuf" else T[name][:] if len(shape) == 2 else T[name][lo]
    return a.bitcast(dt.uint8) if SCRATCH[name][2] == X4 else a


def helper_program(g, core, T, topo):
    n = len(T.cores)
    for r in range(n):
        src = T.cores[r]
        if core not in _helpers(T, topo, src):
            continue
        role = _helpers(T, topo, src).index(core)
        one, two = T.cores[(r + DIST[0]) % n], T.cores[(r + DIST[1]) % n]
        full = len(topo.engines(src, core))
        jobs = [("h0", full // NH, ("hi", 0, 10), ("in4", role, role + 1), "ai1", one)]
        if role == LIST:
            jobs.append(("h1", full, ("ht", 0, 80), ("ml1", 0, 80), "at1", one))
        elif role == SCALES:
            jobs.append(("h1", full, ("hs1", 0, H), ("ss1", 0, H), "as1", one))
            jobs.append(("h3", full, ("ho", 0, 20), ("poff1", 0, 20), "ao", one))
        else:
            lo, hi = RUNS[role - CODES_A]
            jobs.append(("h1", full, ("hc", 0, hi - lo), ("sc1", lo, hi), ("aq1", "ar1")[role - CODES_A], one))
        if role == LIST:
            lo, hi = RUNS[0]
            jobs.append(("h2", len(_spare(topo, src, core, two)), ("hc2", 0, hi - lo), ("sc2", lo, hi), "aq2", two))
        if role == CODES_A:
            jobs.append(("h2", len(_spare(topo, src, core, two)), ("hs2", 0, H), ("ss2", 0, H), "as2", two))
        sent = 0
        for sem, val, a, b, far, dst in jobs:
            rid, pid = topo.addr(dst, core)
            g.wait_ge(T.sem[sem], val)
            g.remote_dma(_raw(T, *b), _raw(T, *a), T.sem[far], T.sem.sent, pid, rid, topo.mask(core, dst))
            sent += len(topo.engines(core, dst))
        g.wait_ge(T.sem.sent, sent)


def rank_program(g, core, T, topo):
    rank = T.rank_of(core)
    if rank is None:
        return helper_program(g, core, T, topo)
    n = len(T.cores)
    A, ACT = AluOpType, ActivationFunctionType
    Q = {"pe": g.tensor, "ve": g.vector, "ac": g.scalar, "gp": g, "sy": g.sync}
    known = {q: {} for q in Q}
    count = {"pe": 0, "ve": 0, "ac": 0, "gp": 0, "dma": 0, "sent": 0}
    hist, last, waited = {}, {}, {}

    def V(name, lo=0, hi=None, step=1):
        return (name, lo, SCRATCH[name][1][1] if hi is None else hi, step)

    def ap(v):
        return T[v[0]][:, v[1]:v[2]] if v[3] == 1 else T[v[0]][:, v[1]:v[2]:v[3]]

    def cols(v):
        if v[0] == "ps":
            return {v[1] // 512}
        return set(range(v[1], v[2], v[3]))

    def wait(q, toks):
        need = {}
        for t in toks:
            if known[q].get(t[0], 0) < t[1] and need.get(t[0], (0, 0))[1] < t[1]:
                need[t[0]] = t
        for t in need.values():
            if known[q].get(t[0], 0) < t[1]:
                Q[q].wait_ge(T.sem[t[0]], t[1])
                waited[t[0]] = max(waited.get(t[0], 0), t[1])
                known[q][t[0]] = t[1]
                for s, val in t[2].items():
                    known[q][s] = max(known[q].get(s, 0), val)

    def note(v, kind, tok, q):
        hist.setdefault(v[0], []).append((cols(v), kind, tok, q))

    def op(q, fn, reads, writes, dma=False):
        deps = []
        for v, w in [(v, False) for v in reads] + [(v, True) for v in writes]:
            c = cols(v)
            for hc, kind, tok, hq in hist.get(v[0], []):
                if (w or kind == "w" or (v[0] == "ps" and hq != q)) and not c.isdisjoint(hc):
                    deps.append(tok)
        wait(q, deps)
        ins = fn()
        if ins is None:
            return None
        if dma:
            sem, val = "d%d" % count["dma"], 16
            count["dma"] += 1
            ins.then_inc(T.sem[sem], 16)
        else:
            count[q] += 1
            sem, val = q, count[q]
            ins.then_inc(T.sem[sem], 1)
        tok = (sem, val, dict(known[q]))
        last[sem] = val
        for v in reads:
            note(v, "r", tok, q)
        for v in writes:
            note(v, "w", tok, q)
        return tok

    def arrives(v, sem, val):
        last[sem] = val
        note(v, "w", (sem, val, {}), "far")

    def is_view(s):
        return isinstance(s, tuple)

    def sc(s):
        return ap(s) if is_view(s) else s

    def gat(win, off):
        return ap(win).indirect(ap(off))

    def memset(o, c):
        op("ve", lambda: g.vector.memset(ap(o), c), [], [o])

    def copy(o, i):
        op("ve", lambda: g.vector.tensor_copy(ap(o), ap(i)), [i], [o])

    def ts(o, i, s1, o0, s2=None, o1=None, off=None):
        r = [i] + [s for s in (s1, s2, off) if is_view(s)]
        src = (lambda: ap(i)) if off is None else (lambda: gat(i, off))
        if o1 is None:
            op("ve", lambda: g.vector.tensor_scalar(ap(o), src(), sc(s1), None, o0), r, [o])
        else:
            op("ve", lambda: g.vector.tensor_scalar(ap(o), src(), sc(s1), sc(s2), o0, o1), r, [o])

    def tt(o, a, b, alu, off=None):
        if off is None:
            op("ve", lambda: g.vector.tensor_tensor(ap(o), ap(a), ap(b), alu), [a, b], [o])
        else:
            op("ve", lambda: g.vector.tensor_tensor(ap(o), gat(a, off), ap(b), alu), [a, b, off], [o])

    def scan(o, a, b, init, o0, o1):
        op("ve", lambda: g.vector.tensor_tensor_scan(ap(o), ap(a), ap(b), init, o0, o1), [a, b], [o])

    def act(o, i, scale=None, off=None, bias=None, func=None):
        r = [i] + [s for s in (off, bias) if is_view(s)]
        src = (lambda: ap(i)) if off is None else (lambda: gat(i, off))
        if bias is not None:
            op("ac", lambda: g.scalar.activation(ap(o), src(), func or ACT.Identity, bias=sc(bias), scale=scale), r, [o])
        elif scale is None:
            op("ac", lambda: g.scalar.activation(ap(o), src(), ACT.Copy), r, [o])
        else:
            op("ac", lambda: g.scalar.activation(ap(o), src(), ACT.Copy, scale=scale), r, [o])

    def quant(c, s, i):
        op("ve", lambda: g.vector.quantize_mx(ap(c), ap(s), ap(i)), [i], [c, s])

    def bank(b, w):
        return V("ps", 512 * b, 512 * b + w)

    def window(r):
        return 128 * (1 - r)

    def valid(b, r):
        lo_, hi_ = RUNS[r]
        return V("ps", 512 * b + PAD + lo_ - window(r), 512 * b + PAD + hi_ - window(r))

    def mm(b, lc, ls, rc, rs):
        o = bank(b, rc[2] - rc[1])
        op("pe", lambda: g.tensor.matmul_mx(ap(o), ap(lc), ap(ls), ap(rc), ap(rs), True, True), [lc, ls, rc, rs], [o])

    def pick_codes(o, win, off):
        op("ve", lambda: g.vector.tensor_copy(ap(o).bitcast(dt.uint32), ap(win).bitcast(dt.uint32).indirect(ap(off))), [win, off], [o])

    def iota(o, pattern, base, cm):
        if SCRATCH[o[0]][2] == I32:
            op("gp", lambda: g.iota(ap(o), pattern, base, cm), [], [o])
        else:
            op("gp", lambda: g.iota(ap(o), pattern, base, cm, allow_small_or_imprecise_dtypes=True), [], [o])

    def dma(q, out, in_, reads, writes):
        return op(q, lambda: Q[q].dma_start(out, in_), reads, writes, dma=True)

    def send(src, dst, to, sem, engines):
        rid, pid = topo.addr(to, core)

        def fn():
            g.remote_dma(_raw(T, *dst[:3]), _raw(T, *src[:3]), T.sem[sem], T.sem.sent, pid, rid, _bits(engines))
        op("gp", fn, [src], [])
        count["sent"] += len(engines)

    def spread(srcs, dst, tos, sem):
        eng = topo.engines(core, tos[0])
        w = len(eng) // len(tos)

        def fn():
            tr = []
            for s, to in enumerate(tos):
                rid, pid = topo.addr(to, core)
                tr.append(RemoteDMATransfer(dst_ids=[DstId(rid=rid, pnc=pid)], dma_engine_mask=_bits(eng[w * s:w * s + w]),
                                            remote_sem=T.sem[sem], src=_raw(T, *srcs[s][:3]), dst=_raw(T, *dst[:3])))
            g.remote_dma_fused(tr, local_sem=T.sem.sent)
        op("gp", fn, srcs, [])
        count["sent"] += len(eng)

    def col(k):
        return V("cf", k, k + 1)

    def E(b):
        return V("ec", 128 * b, 128 * b + 128), V("es", 128 * b, 128 * b + 128)

    def hold_pattern(o, t, start):
        yield act(V("ha"), t, -1.0, bias=start, func=ACT.Relu)
        yield act(V("hb"), V("ha"), 1.0, bias=-0.75, func=ACT.Square)
        yield act(o, V("hb"), -2 * KEEP, bias=2 * KEEP * 0.5625)

    dma("ac", T.stage[:, 0:C], T.li[:], [], [V("stage", 0, C)])
    dma("sy", T.stage[:, C:2 * C], T.ri[:], [], [V("stage", C, 2 * C)])
    dma("ac", T.ut[:], T.u[:], [], [V("ut")])
    xin = dma("sy", T.xt[:], T.x[:], [], [V("xt")])
    dma("ac", T.out4[0:2], T.li[:], [], [V("out4", 0, 2)])
    dma("ac", T.out4[2:4], T.ri[:], [], [V("out4", 2, 4)])
    wait("sy", [xin])
    min_ = dma("sy", T.mt[:], T.mid[:], [], [V("mt")])
    wait("sy", [min_])
    dma("sy", T.wq[:].bitcast(dt.uint8), T.wc[:], [], [V("wq")])
    dma("sy", T.wp[:], T.ws[:], [], [V("wp")])
    dma("sy", T.vt[:], T.v[:], [], [V("vt")])

    I16, I8, T2, I20, FIRST, LAST, J1, START16, NOFF, P20, P16, FO = 0, 1, 2, 5, 6, 7, 8, 9, 11, 12, 13, 15
    memset(V("eye"), 0.0)
    iota(V("pp"), [[0, 2]], 0, 1)
    iota(V("c16"), [[16, 20]], 0, 0)
    diag = V("eye", 3, 515, 4)
    op("gp", lambda: g.affine_select(ap(diag), ap(diag), [[1, 128]], A.not_equal, 1.0, 0, -1), [diag], [diag])
    iota(V("t16"), [[0, H // 16 + 1], [1, 16]], 0, 0)
    p = V("pp", 0, 1)
    memset(V("cs1", 0, 2), 0.0)
    memset(V("cs2", 0, 2), 0.0)
    ts(V("ci", 0, 1), p, 15, A.bitwise_and)
    ts(V("ci", 1, 2), p, 1, A.arith_shift_right, 7, A.bitwise_and)
    ts(V("ci", 2, 3), p, 1, A.bitwise_and)
    ts(V("ci", 3, 4), p, 4, A.arith_shift_right)
    copy(V("uo"), V("c16", 0, 8))
    memset(V("d1"), LOW)
    memset(V("ml0"), LOW)
    copy(V("cf", 0, 3), V("ci", 0, 3))
    memset(V("ms1"), LOW)
    memset(V("d1", 2, 80, 4), 0.0)
    ts(col(FIRST), col(I16), 0.0, A.is_equal, 16.0, A.mult)
    ts(col(LAST), col(I16), 15.0, A.is_equal, KEEP, A.mult)
    for b in range(4):
        quant(*E(b), V("eye", 3 - b, 515 - b))
    act(col(START16), col(I16), 1.0, bias=2.0)
    act(col(I20), col(I16), 20.0)
    act(col(J1), col(FIRST), 2.0, bias=col(I16))
    act(col(NOFF), col(T2), float(NM))
    act(col(P20), col(LAST), 20.0, bias=20 * (H - KEEP) + WHOLE * (C - 1))
    act(col(P16), col(LAST), 1.0, bias=H - KEEP - 7.5 + 16 * WHOLE)
    gi = V("ci", 3, 4)

    def repeat(o, src):
        op("gp", lambda: g.indirect_dma_start(T[o][:], None, T[src][:], IndirectOffsetOnAxis(ap=ap(gi), axis=0), bounds_check=7),
           [V(src), gi], [V(o)], dma=True)

    hop = _helpers(T, topo, core)
    far = len(topo.engines(hop[0], T.cores[(rank + DIST[0]) % n]))
    repeat("lr0", "stage")
    iota(V("val1"), [[1, C]], -H, 0)
    iota(V("t8"), [[0, H // 8], [1, 8]], 0, 0)
    spread([V("out4", s, s + 1) for s in range(NH)], V("hi"), hop, "h0")
    arrives(V("in4", 0, NH), "ai1", NH * far)
    dma("sy", T.stage1[:, 0:C], T.in4[0:2], [V("in4", 0, 2)], [V("stage1", 0, C)])
    dma("sy", T.stage1[:, C:2 * C], T.in4[2:4], [V("in4", 2, 4)], [V("stage1", C, 2 * C)])
    iota(V("val2"), [[C, 2], [1, H]], -240, 0)

    quant(V("uc0"), V("us0"), V("ut"))
    ts(V("d1", 0, 80, 4), V("c16"), col(J1), A.add)
    memset(V("ms1", 2, 40, 4), 0.0)
    memset(V("pa"), 0.0)
    pick_codes(V("uc1"), V("uc0"), V("uo"))
    act(V("us1"), V("us0"), off=V("uo"))
    memset(V("zt", 0, 4 * PAD), 0.0)
    memset(V("zt", 4 * (PAD + H)), 0.0)
    list(hold_pattern(V("h16"), V("t16", 0, H), col(START16)))
    for s in range(2):
        quant(V("xc", H * s, H * s + H), V("xs", H * s, H * s + H), V("xt", 4 * H * s, 4 * H * s + 4 * H))
        mm(4 + s, V("uc1"), V("us1"), V("xc", H * s, H * s + H), V("xs", H * s, H * s + H))
    ts(V("mk"), V("t16"), col(I16), A.is_equal, 16 * UNIT, A.mult)
    memset(V("vv", 0, 4 * PAD), 0.0)
    memset(V("vv", 4 * (PAD + H)), 0.0)
    for b in range(4):
        mm(b, *E(b), V("xc"), V("xs"))

    def unpack_x(b):
        act(V("ff", C * b, C * b + C), bank(b, C), 0.5)

    def flags(lo_, hi_, src):
        ts(V("fl", lo_, hi_), src, 0.0, A.is_gt, UNIT / 2, A.mult)

    def running(cs, lo_):
        scan(V(cs, 2, H + 2), V("fl", lo_, lo_ + H), V("fl", lo_, lo_ + H), 0.0, A.add, A.add)

    def held_counts(cs, at):
        scan(V("hd", at + H, at + C), V(cs, 1, H + 1), V("mk", 1, H + 1), 1e6, A.min, A.add)
        scan(V("hd", at, at + H), V(cs, 2, H + 2), V("mk", 1, H + 1), 1e6, A.min, A.add)
        return V("hd", at + H + 15, at + C, 16), V("hd", at + 15, at + H, 16)

    flags(0, H, bank(4, H))
    flags(H, C, bank(5, H))
    running("cs1", 0)
    ts(V("ro"), V("c16"), 1.0 / 16, A.mult, col(I20), A.add)
    running("cs2", H)
    first, second = V("cs1", H + 1, H + 2), V("cs2", H + 1, H + 2)
    unpack_x(0)
    act(V("tc", 2, 3), first, 1 / UNIT)
    act(V("tc", 1, 2), second, 1 / UNIT)
    act(V("tc", 0, 1), second, 1 / UNIT, bias=V("tc", 2, 3))
    counts = [held_counts("cs1", 0), held_counts("cs2", C)]
    ts(V("d1", 42, 80, 4), V("d1", 2, 40, 4), V("tc", 2, 3), A.add)
    for s in (1, 0):
        act(V("ml0", 40 * s + 1, 40 * s + 40, 4), counts[s][0], -2 / UNIT, bias=V("tc", s, s + 1))
    for s in range(2):
        ts(V("ml0", 40 * s + 3, 40 * s + 40, 4), counts[s][0], 1 / UNIT, A.mult)
        tt(V("ml0", 40 * s + 2, 40 * s + 40, 4), *counts[s], A.subtract)
    for b in range(1, 4):
        unpack_x(b)

    for k in range(1, len(DIST) + 1):
        end = k == len(DIST)
        to, frm = T.cores[(rank + DIST[k - 1]) % n], T.cores[(rank - DIST[k - 1]) % n]
        assert topo.may_write(core, to) == (k > 1) and len(hop) == NH
        ab, nab, qc, qs = "ab%d" % (k - 1), "ab%d" % k, "sc%d" % k, "ss%d" % k
        if k == 1:
            fwin = [V("ff", C * b, C * b + C) for b in range(4)]
            awin, bwin, vals, back = V(ab, 0, C), V(ab, C, 2 * C), V("val1"), float(H)
        else:
            fwin = [V("ff", s, s + 3 * H) for s in (0, H, 4 * H, 5 * H)]
            awin, bwin, vals, back = V(ab, 0, 3 * H), V(ab, H, 4 * H), V("val2"), 240.0
        scan(V("pf"), V("ml%d" % (k - 1)), V("d1"), 0.0, A.add, A.max)
        if k == 1:
            quant(V("mc"), V("ms"), V("mt"))
            ts(V("qa"), V("t8"), col(I8), A.is_equal, UNIT, A.mult)
        ts(V("pos"), V("pf", 3, 80, 4), col(FIRST), A.subtract)
        if k == 1:
            memset(V("pb"), 1.0 - C)
            memset(V("nb", 1, C, 2), -UNIT)
            act(V("qb"), V("qa"), 2.0, bias=-UNIT)
            act(V("na", 0, C, 2), V("qa"), -1.0)
            for b in range(4):
                mm(4 + b, *E(b), V("mc"), V("ms"))
            act(V(ab, C, 2 * C), V("lr0", C, 2 * C), float(NI), off=V("ro"))
            act(V(ab, 0, C), V("lr0", 0, C), off=V("ro"))

        def unpack_mid(*planes):
            for s in planes if k == 1 else ():
                ts(V("mh", NM * s, NM * s + NM), bank(4 + PLANES[s], NM), 0.5, A.mult)

        op("ve", lambda: g.vector.tensor_copy(gat(V("oo"), V("pos")), ap(vals)), [vals, V("pos")], [V("oo")])
        unpack_mid(0, 1)
        for s in range(2):
            scan(V("ee", H * s, H * s + H), V("h16"), V("oo", s, C, 2), 0.0, A.add, A.max)
        unpack_mid(2)
        lo, ho = V("off", 0, 10), V("off", 10, 20)
        ts(lo, V("ee", 15, H, 16), col(LAST), A.add, back - KEEP, A.add)
        ts(ho, V("ee", H + 15, C, 16), col(LAST), A.add, back - KEEP, A.add)
        unpack_mid(3)

        def left(b):
            act(V("ll", H * b, H * b + H), fwin[b], off=lo)

        def larger(b):
            tt(V("ph", b, 4 * H, 4), fwin[b], V("ll", H * b, H * b + H), A.max, off=ho)

        def middle(step):
            if step == 1:
                scan(V("n2"), V("na"), V("nb"), 0.0, A.add, A.max)
            else:
                ts(V("noff"), V("n2", 15, C, 16), col(NOFF), A.add)

        tt(V("nb", 0, C, 2), bwin, V("qb"), A.min, off=lo)
        tt(V("na", 1, C, 2), awin, V("qa"), A.min, off=ho)
        for b in PLANES:
            left(b)
        act(V("rr"), fwin[PLANES[3]], off=ho)
        for s, b in enumerate(PLANES[:3]):
            larger(b)
            if s < 2:
                middle(s + 1)
        tt(V("ph", PLANES[3], 4 * H, 4), V("rr"), V("ll", H * PLANES[3], H * PLANES[3] + H), A.max)
        act(V(nab, 0, H), awin, off=lo)
        for r, s in PICKED:
            lo_, hi_ = RUNS[r]
            act(V("mg", 4 * lo_ + s, 4 * hi_, 2), V("mh", 2 * NM * s, 2 * NM * s + 2 * NM), off=V("noff", lo_ // 8, hi_ // 8))
        act(V(nab, H, C), bwin, off=ho)
        far = len(topo.engines(hop[0] if k == 1 else core, to))
        if 1 < k < len(DIST):
            send(V(nab, 0, C), V(nab, C, 2 * C), to, "ai%d" % k, topo.engines(core, to))
            arrives(V(nab, C, 2 * C), "ai%d" % k, far)
        elif end:
            dma("sy", T.fold[:], T[nab][0:128:16, :], [V(nab)], [V("fold")])
            dma("sy", T.tb[0:8, 0:C], T[nab][0:128:16, :], [V(nab)], [V("tb", 0, C)])
            send(V("fold"), V("land"), to, "ai%d" % k, topo.engines(core, to))
            arrives(V("land"), "ai%d" % k, far)
            dma("sy", T.tb[0:8, C:2 * C], T.land[:], [V("land")], [V("tb", C, 2 * C)])
        def middle_sum(r, s):
            lo_, hi_ = RUNS[r]
            o, p_ = V("zt", 4 * (PAD + lo_) + s, 4 * (PAD + hi_), 2), V("ph", 4 * lo_ + s, 4 * hi_, 2)
            if (r, s) in PICKED:
                tt(o, V("mg", 4 * lo_ + s, 4 * hi_, 2), p_, A.add)
            else:
                tt(o, V("mh", 2 * NM * s, 2 * NM * s + 2 * NM), p_, A.add, off=V("noff", lo_ // 8, hi_ // 8))

        def larger32(r):
            lo_, hi_ = RUNS[r]
            ts(V("p32", 4 * lo_, 4 * hi_), V("ph", 4 * lo_, 4 * hi_), 64.0, A.mult)

        def layer(r):
            w = window(r)
            quant(V("zc", w, w + 128), V("zs", w, w + 128), V("zt", 4 * w, 4 * w + 512))
            for b in range(4):
                mm(4 * r + b, V("wq", 128 * b, 128 * b + 128), V("wp", 128 * b, 128 * b + 128), V("zc", w, w + 128), V("zs", w, w + 128))

        def add_larger(r):
            lo_, hi_ = RUNS[r]
            for b in range(4):
                sums = V("v32", H * b + lo_, H * b + hi_)
                tt(sums, valid(4 * r + b, r), V("p32", 4 * lo_ + b, 4 * hi_, 4), A.add)
                act(V("vv", 4 * (PAD + lo_) + b, 4 * (PAD + hi_), 4), sums, 1.0 / 32)

        def new_half(r):
            w = window(r)
            c, s = V(qc, H + w, H + w + 128), V(qs, H + w, H + w + 128)
            quant(c, s, V("vv", 4 * w, 4 * w + 512))
            mm(4 * r, *((V("vc"), V("vs")) if end else (V("uc1"), V("us1"))), c, s)

        def send_codes(r):
            lo_, hi_ = RUNS[r]
            sem = ("aq%d", "ar%d")[r] % k
            if k == 1:
                send(V(qc, OWN + lo_, OWN + hi_), V("hc", 0, hi_ - lo_), hop[CODES_A + r], "h1", topo.engines(core, hop[CODES_A + r]))
            elif not end and r == 0:
                send(V(qc, OWN + lo_, OWN + hi_), V("hc2", 0, hi_ - lo_), hop[LIST], "h2", _spare(topo, core, hop[LIST], to))
            else:
                send(V(qc, OWN + lo_, OWN + hi_), V(qc, lo_, hi_), to, sem, topo.engines(core, to))
            arrives(V(qc, lo_, hi_), sem, far)

        oc, os_, rc, rs = V(qc, OWN, OWN + H), V(qs, OWN, OWN + H), V(qc, 0, H), V(qs, 0, H)
        held = V("ee", 15, C, 16)
        middle_sum(0, 0)
        middle_sum(0, 1)
        middle_sum(1, 0)
        middle_sum(1, 1)
        layer(0)
        larger32(0)
        layer(1)
        larger32(1)
        add_larger(0)
        add_larger(1)
        if k == 1:
            ts(V("pa", 1, 40, 2), held, col(P16), A.add, 1.0 / 16, A.mult)
            ts(V("pb", 1, 40, 2), held, 20.0, A.mult, col(P20), A.add)
        new_half(0)
        send_codes(0)
        if k == 1:
            scan(V("pc"), V("pa"), V("pb"), 0.0, A.mult, A.add)
        new_half(1)
        if end:
            send(os_, rs, to, "as%d" % k, topo.engines(core, to))
        send_codes(1)
        if k == 1:
            send(os_, V("hs1"), hop[SCALES], "h1", topo.engines(core, hop[SCALES]))
            copy(V("poff"), V("pc", 1, 40, 2))
        elif not end:
            send(os_, V("hs2"), hop[CODES_A], "h2", _spare(topo, core, hop[CODES_A], to))
        arrives(rs, "as%d" % k, far)
        if end:
            break
        ms, ml = "ms%d" % k, "ml%d" % k
        for b in range(4):
            mm(UNPACK[0][b], *E(b), oc, os_)
        for r in range(2):
            flags(*RUNS[r], valid(4 * r, r))
        if k == 1:
            ts(col(17), col(FIRST), 1.5, A.mult, col(I16), A.add)
            memset(V("ms2"), LOW)
            ts(col(FO), col(T2), float(OWN), A.mult, col(I8), A.add)
        running("cs2", 0)
        if k == 1:
            ts(V("j2", 10, 20), V("c16", 0, 10), col(17), A.add, 2.0, A.mult)
            memset(V("ms2", 2, 40, 4), 0.0)
        act(V("tc", 1, 2), second, 1 / UNIT)
        without, with_ = held_counts("cs2", 0)
        hb = V("hd", 15, 2 * H, 16)
        act(V(ms, 1, 80, 4), hb, -2 / UNIT, bias=V("tc", 1, 2))
        ts(V(ms, 3, 80, 4), hb, 1 / UNIT, A.mult)
        tt(V(ms, 42, 80, 4), without, with_, A.subtract)
        if k == 1:
            send(V(ms), V("ht"), hop[LIST], "h1", topo.engines(core, hop[LIST]))
            send(V("poff"), V("ho"), hop[SCALES], "h3", topo.engines(core, hop[SCALES]))
            arrives(V("poff1"), "ao", far)
            repeat("lr1", "stage1")
        else:
            send(V(ms), V(ml), to, "at%d" % k, topo.engines(core, to))
        arrives(V(ml), "at%d" % k, far)
        at = (0, H, 4 * H, 5 * H)
        for b in range(4):
            act(V("ff", at[b], at[b] + H), bank(UNPACK[0][b], H), 0.5)
        if k == 1:
            ts(V("j2", 0, 10), V("j2", 10, 20), 1.0, A.add)
        tt(V("tq", 0, 10), V(ms, 41, 80, 4), V(ms, 43, 80, 4), A.add)
        for s in range(2):
            ts(V("d1", 40 * s + 2, 40 * s + 40, 4), V(ms, 43, 80, 4), col(FIRST), A.subtract)
        tt(V("d1", 40, 80, 4), V("tq", 0, 10), V("j2", 10, 20), A.add)
        tt(V("tq", 10, 20), V("tq", 0, 10), V("j2", 0, 10), A.add)
        tt(V("d1", 0, 40, 4), V("tq", 10, 20), V(ms, 42, 80, 4), A.add)
        if k == 1:
            quant(V("vc"), V("vs"), V("vt"))
            ts(V("tq"), V("c16"), 0.5, A.mult, col(FO), A.add)
            for lo_, hi_ in RUNS:
                ts(V("fo", lo_ // 8, hi_ // 8), V("tq", lo_ // 8, hi_ // 8), -float(lo_), A.add)
        for b in range(4):
            mm(UNPACK[1][b], *E(b), rc, rs)
        for b in range(4):
            act(V("ff", at[b] + 2 * H, at[b] + 3 * H), bank(UNPACK[1][b], H), 0.5)
        if k == 1:
            act(V(nab, 3 * H, 4 * H), V("lr1", C, 2 * C), float(NI), off=V("poff1", 10, 20))
            act(V(nab, 2 * H, 3 * H), V("lr1", 0, C), off=V("poff1", 0, 10))

    for r, (lo_, hi_) in enumerate(RUNS):
        act(V("yy", 2 * lo_ + 1, 2 * hi_, 2), valid(4 * r, r))

    def last_indices(own):
        for s in range(2):
            lo, at = C * (1 - own) + H * s, C * s + own
            op("ve", lambda: g.vector.tensor_scalar(T.lro[0:8, at:C * s + C:2], T.tb[0:8, lo:lo + H], (1.0, 1.0 / NI)[s], None, A.mult),
               [V("tb", lo, lo + H)], [V("lro", at, C * s + C, 2)])

    last_indices(1)
    for r, (lo_, hi_) in enumerate(RUNS):
        a, b = 2 * lo_, 2 * hi_
        pick_codes(V("pkc", a, b), V(qc, lo_), V("fo", lo_ // 8, hi_ // 8))
        dma("sy", T.oc[:, 4 * a:4 * b], T.pkc[:, a:b].bitcast(dt.uint8), [V("pkc", a, b)], [])
        mm(1 + r, V("vc"), V("vs"), V(qc, lo_, lo_ + 128), V(qs, lo_, lo_ + 128))
        act(V("yy", a, b, 2), bank(1 + r, hi_ - lo_))
        dma("ac", T.y[:, a:b], T.yy[:, a:b], [V("yy", a, b)], [])
        if r == 0:
            for lo2, hi2 in RUNS:
                o, win, off = V("pks", 2 * lo2, 2 * hi2), V(qs, lo2), V("fo", lo2 // 8, hi2 // 8)
                op("ve", lambda: g.vector.tensor_copy(ap(o), gat(win, off)), [win, off], [o])
            for a in range(4):
                dma("sy", T.osc[4 * a:4 * a + 4, 0:C], T.pks[32 * a:32 * a + 4, 0:C], [V("pks")], [])
    last_indices(0)
    dma("sy", T.lr[:], T.lro[0:8, :], [V("lro")], [])
    last["sent"] = count["sent"]
    for s, val in last.items():
        if waited.get(s, 0) < val:
            g.wait_ge(T.sem[s], val)
